import numpy as np
import ml_dtypes


def mxq(x, axis, fmt="e4m3"):
    dtype, down = {"e4m3": (ml_dtypes.float8_e4m3fn, 7), "e5m2": (ml_dtypes.float8_e5m2, 14)}[fmt]
    v = np.moveaxis(np.asarray(x, np.float32).astype(ml_dtypes.bfloat16).astype(np.float64), axis, -1)
    blocks = v.reshape(v.shape[:-1] + (-1, 32))
    amax = np.abs(blocks).max(-1, keepdims=True)
    byte = np.maximum(np.where(amax > 0, np.frexp(amax)[1] - 1 + 127, 0) - down, 1)
    scale = np.exp2(byte - 127.0)
    codes = (blocks / scale).astype(np.float32).astype(dtype).astype(np.float64)
    return np.moveaxis((codes * scale).reshape(v.shape), -1, axis)


WIDE = False


def mx_kscale(k):
    if not WIDE:
        return np.ones(k)
    levels = np.array([30, -30])
    if k % 512:
        return np.exp2(np.random.permutation(np.resize(levels, k // 32))).repeat(32)
    a = np.empty((k // 512, 16))
    for p in range(k // 512):
        a[p, :8] = np.random.permutation(np.resize(levels, 8))
        for g in range(8):
            far = levels[np.abs(levels - a[p, g]) >= 10]
            a[p, g + 8] = far[np.random.randint(len(far))]
    return np.exp2(a.ravel()).repeat(32)


def f64(x):
    return np.asarray(x).astype(np.float64)


E2M1 = np.array([0.0, 0.5, 1.0, 1.5, 2.0, 3.0, 4.0, 6.0, -0.0, -0.5, -1.0, -1.5, -2.0, -3.0, -4.0, -6.0])


def pack_weight(w, fmt):
    k, n = w.shape
    w = f64(np.asarray(w, np.float32).astype(ml_dtypes.bfloat16)).reshape(k // 32, 32, n)
    amax = np.abs(w).max(1)
    if fmt == "e4m3":
        byte = np.frexp(amax)[1] - 1 + 127 - 7
    else:
        mant, ex = np.frexp(amax / 6.0)
        byte = np.where(mant > 0.5, ex, ex - 1) + 127
    byte = np.clip(np.where(amax > 0, byte, 1), 1, 254)
    scaled = (w * np.exp2(127.0 - byte)[:, None, :]).reshape(k, n).astype(np.float32)
    by_word = np.ascontiguousarray(scaled.reshape(k // 512, 128, 4, n).transpose(0, 1, 3, 2))
    if fmt == "e4m3":
        words = by_word.astype(ml_dtypes.float8_e4m3fn).view(np.uint8)
    else:
        c = by_word.astype(ml_dtypes.float4_e2m1fn).view(np.uint8) & 0xF
        words = (c[..., 0::2] | (c[..., 1::2] << 4)).reshape(k // 512, 128, 2 * n)
    return np.ascontiguousarray(words), np.ascontiguousarray(byte.astype(np.uint8).reshape(k // 512, 16, n))


def unpack_weight(words, scales, fmt):
    g, _, n = scales.shape
    words = np.ascontiguousarray(words).reshape(g, 128, n, -1)
    if fmt == "e4m3":
        vals = words.view(ml_dtypes.float8_e4m3fn).astype(np.float64)
    else:
        nib = np.empty((g, 128, n, 4), np.uint8)
        nib[..., 0::2] = words & 0xF
        nib[..., 1::2] = words >> 4
        vals = E2M1[nib]
    vals = vals * np.repeat(np.exp2(scales.astype(np.float64) - 127.0), 8, axis=1)[..., None]
    return vals.transpose(0, 1, 3, 2).reshape(g * 512, n)


K, O, T, R, N = 1024, 1024, 1024, 512, 1536


def setup_inputs():
    n = np.random.standard_normal
    s = mx_kscale(K)[:, None]
    u = mx_kscale(T)[:, None]
    m = np.exp(0.5 * n((O + T, 1)))
    ux = mx_kscale(O)[:, None]
    p_hs = pack_weight(n((O, R)) * ux, "e4m3")
    return {
        "x": (n((K, T)) * s * u.T).astype(np.float32),
        "dn": (n((K, R)) / np.sqrt(K) / s).astype(np.float32),
        "hs_words": p_hs[0],
        "hs_scales": p_hs[1],
        "dy0": (m[:O] * n((O, N)) / np.sqrt(O + T) / ux).astype(np.float32),
        "dy1": (m[O:] * n((T, N)) / np.sqrt(O + T) / u).astype(np.float32),
        "mom": (n((R, N))).astype(np.float32),
    }


def reference(x, dn, hs_words, hs_scales, dy0, dy1, mom):
    x_ = mxq(f64(x), 0, "e4m3")
    dn_ = mxq(f64(dn), 0, "e4m3")
    h = x_.T @ dn_
    h_ = mxq(h, 0, "e4m3")
    hs_ = unpack_weight(hs_words, hs_scales, "e4m3")
    dy0_ = mxq(f64(dy0), 0, "e5m2")
    dy1_ = mxq(f64(dy1), 0, "e5m2")
    db = hs_.T @ dy0_ + h_.T @ dy1_
    return 0.9 * f64(mom) + db

@@ -1,0 +1,173 @@
+from contextlib import ExitStack
+
+import concourse.mybir as mybir
+
+K, O, T, R, N = 1024, 1024, 1024, 512, 1536
+FLOPS = 2 * K * T * R + 2 * (O + T) * R * N
+
+F32 = mybir.dt.float32
+BF16 = mybir.dt.bfloat16
+U32 = mybir.dt.uint32
+I32 = mybir.dt.int32
+U8 = mybir.dt.uint8
+E4M3 = mybir.dt.float8_e4m3fn_x4
+E5M2 = mybir.dt.float8_e5m2_x4
+ALU = mybir.AluOpType
+
+P = 128
+PACK = 4
+ROWS = P * PACK
+COLS = 512
+SCALAR_COLS = 256
+SCALAR_COLS_LAST = 176
+R_TILES = R // P
+N_CHUNKS = N // COLS
+BANKS = 8
+
+
+def tile_mix_lorab_ema_kernel(tc, x, dn, hs_words, hs_scales, dy0, dy1, mom, out):
+    nc = tc.nc
+
+    with ExitStack() as ctx:
+        keep = ctx.enter_context(tc.tile_pool(name="keep", bufs=1))
+        wide = ctx.enter_context(tc.tile_pool(name="wide", bufs=4))
+        stage = ctx.enter_context(tc.tile_pool(name="stage", bufs=6))
+        psum = ctx.enter_context(tc.psum_pool(name="psum", bufs=BANKS))
+        ctx.enter_context(tc.manual_schedule())
+
+        def load_pass(pool, name, tag, src, a):
+            width = src.shape[1]
+            raw = pool.tile([P, PACK, width], F32, name=name, tag=tag)
+            nc.sync.dma_start(out=raw[:], in_=src[a * ROWS : (a + 1) * ROWS, :].rearrange("(p j) w -> p j w", j=PACK))
+            return raw
+
+        def new_stage():
+            grouped = stage.tile([P, COLS, PACK], BF16, name="grouped", tag="grouped", align_bytes=64)
+            return grouped
+
+        def interleave(copy, grouped, raw, first, lo, hi):
+            copy(
+                out=grouped[:, lo:hi, :].rearrange("p (c i) j -> p c j i", i=4),
+                in_=raw[:, :, first + lo : first + hi].rearrange("p j (c i) -> p c j i", i=4),
+            )
+
+        def interleave_permuted(copy, grouped, raw, first):
+            copy(
+                out=grouped[:].rearrange("p (s m) j -> p m j s", s=PACK),
+                in_=raw[:, :, first : first + COLS].rearrange("p j (m s) -> p m j s", s=PACK),
+            )
+
+        def quantize(name, grouped, fmt):
+            codes = keep.tile([P, COLS], U32, name=name + "_codes", align_bytes=64)
+            scales = keep.tile([P, COLS], U8, name=name + "_scales", align_bytes=64)
+            nc.vector.quantize_mx(out=codes[:].bitcast(fmt), scales=scales[:], in_=grouped[:].rearrange("p c j -> p (c j)"))
+            return codes, scales
+
+        def mx_pass(acc, stationary, m0, moving, n0, n, moving_fmt, start, stop):
+            nc.tensor.matmul_mx(
+                out=acc,
+                lhsT=stationary[0][:, m0 : m0 + P].bitcast(E4M3),
+                lhsT_scale=stationary[1][:, m0 : m0 + P],
+                rhs=moving[0][:, n0 : n0 + n].bitcast(moving_fmt),
+                rhs_scale=moving[1][:, n0 : n0 + n],
+                start=start,
+                stop=stop,
+            )
+
+        hs_plane = keep.tile([P, 2, R], U8, name="hs_plane", align_bytes=64)
+        nc.gpsimd.memset(hs_plane[:].bitcast(I32), 0)
+        for q in range(4):
+            nc.gpsimd.dma_start(
+                out=hs_plane[32 * q : 32 * q + 4, :, :].bitcast(I32),
+                in_=hs_scales[:, 4 * q : 4 * q + 4, :].rearrange("a r n -> r a n").bitcast(I32),
+            )
+
+        dn_raw, x_raw = [], []
+        for a in range(2):
+            dn_raw.append(load_pass(keep, "dn_raw%d" % a, "dn_raw%d" % a, dn, a))
+            x_raw.append(load_pass(wide, "x_raw%d" % a, "wide", x, a))
+        hs_codes = keep.tile([P, 2, R], U32, name="hs_codes", align_bytes=64)
+        nc.sync.dma_start(out=hs_codes[:].bitcast(I32), in_=hs_words.rearrange("a p r i -> p a (r i)").bitcast(I32))
+        dy_raw = [load_pass(wide, "dy0_raw%d" % a, "wide", dy0, a) for a in range(2)]
+
+        dn_q, x_q = [], []
+        for a in range(2):
+            dn_g = new_stage()
+            interleave(nc.scalar.copy, dn_g, dn_raw[a], 0, 0, SCALAR_COLS)
+            interleave(nc.vector.tensor_copy, dn_g, dn_raw[a], 0, SCALAR_COLS, COLS)
+            dn_q.append(quantize("dn%d" % a, dn_g, E4M3))
+            x_g0 = new_stage()
+            interleave_permuted(nc.vector.tensor_copy, x_g0, x_raw[a], 0)
+            x_g1 = new_stage()
+            interleave_permuted(nc.scalar.copy, x_g1, x_raw[a], COLS)
+            x_q.append([quantize("x%d0" % a, x_g0, E4M3), quantize("x%d1" % a, x_g1, E4M3)])
+            if a == 0:
+                dy_raw.append(load_pass(wide, "dy1_raw0", "wide", dy1, 0))
+        head_cols = N - COLS
+        dy_raw.append(load_pass(wide, "dy1_raw1", "wide", dy1[:, :head_cols], 1))
+        dy_last = load_pass(keep, "dy_last", "dy_last", dy1[:, head_cols:], 1)
+
+        mom_sb = []
+        for r in range(R_TILES):
+            m_tile = keep.tile([P, N], F32, name="mom%d" % r)
+            nc.sync.dma_start(out=m_tile[:], in_=mom[r * P : (r + 1) * P, :])
+            mom_sb.append(m_tile)
+
+        lhs = [(hs_codes[:, a, :], hs_plane[:, a, :]) for a in range(2)]
+        for b in range(2):
+            h_g = new_stage()
+            for r in range(R_TILES):
+                bank = psum.tile([P, COLS], F32, name="h_bank", tag="bank")
+                for s in range(PACK):
+                    for a in range(2):
+                        mx_pass(bank[:, s * P : (s + 1) * P], x_q[a][b], s * P, dn_q[a], r * P, P, E4M3, a == 0, a == 1)
+                nc.scalar.copy(out=h_g[:, r * P : (r + 1) * P, :], in_=bank[:].rearrange("p (s n) -> p n s", s=PACK))
+            lhs.append(quantize("h%d" % b, h_g, E4M3))
+
+        tiles = [(r, c) for r in range(R_TILES) for c in range(N_CHUNKS)]
+        early, late = tiles[:BANKS], tiles[BANKS:]
+        acc = {}
+        dy_q = {}
+
+        def open_tile(rc):
+            bank = psum.tile([P, COLS], F32, name="acc", tag="bank")
+            acc[rc] = bank
+
+        def out_pass(rc, g):
+            r, c = rc
+            mx_pass(acc[rc][:], lhs[g], r * P, dy_q[g, c], 0, COLS, E5M2, g == 0, g == 3)
+
+        def finish(rc):
+            r, c = rc
+            cols = slice(c * COLS, (c + 1) * COLS)
+            nc.vector.scalar_tensor_tensor(
+                out=mom_sb[r][:, cols], in0=mom_sb[r][:, cols], scalar=0.9, in1=acc[rc][:], op0=ALU.mult, op1=ALU.add
+            )
+            if c == N_CHUNKS - 1:
+                nc.sync.dma_start(out=out[r * P : (r + 1) * P, :], in_=mom_sb[r][:])
+
+        for rc in early:
+            open_tile(rc)
+        loads = [(g, dy_raw[g], range(N_CHUNKS), SCALAR_COLS) for g in range(3)]
+        loads.append((3, dy_raw[3], range(N_CHUNKS - 1), SCALAR_COLS))
+        loads.append((3, dy_last, range(N_CHUNKS - 1, N_CHUNKS), SCALAR_COLS_LAST))
+        for g, raw, chunks, split in loads:
+            groups = {}
+            for c in chunks:
+                dy_g = new_stage()
+                first = (c - chunks.start) * COLS
+                interleave(nc.scalar.copy, dy_g, raw, first, 0, split)
+                interleave(nc.vector.tensor_copy, dy_g, raw, first, split, COLS)
+                groups[c] = dy_g
+            for c in chunks:
+                dy_q[g, c] = quantize("dy%d%d" % (g, c), groups[c], E5M2)
+                for rc in early:
+                    if rc[1] == c:
+                        out_pass(rc, g)
+
+        for i, rc in enumerate(tiles):
+            finish(rc)
+            if i < len(late):
+                open_tile(late[i])
+                for g in range(4):
+                    out_pass(late[i], g)

@@ -74,38 +74,35 @@ def tile_mix_lorab_ema_kernel(tc, x, dn, hs_words, hs_scales, dy0, dy1, mom, out
                 stop=stop,
             )
 
+        dn_raw = keep.tile([P, 2, PACK, R], F32, name="dn_raw")
+        nc.sync.dma_start(out=dn_raw[:], in_=dn.rearrange("(a p j) w -> p a j w", a=2, j=PACK))
+        x_raw = [load_pass(wide, "x_raw%d" % a, "wide", x, a) for a in range(2)]
         hs_plane = keep.tile([P, 2, R], U8, name="hs_plane", align_bytes=64)
-        nc.gpsimd.memset(hs_plane[:].bitcast(I32), 0)
+        nc.vector.memset(hs_plane[:].bitcast(I32), 0)
         for q in range(4):
-            nc.gpsimd.dma_start(
+            nc.scalar.dma_start(
                 out=hs_plane[32 * q : 32 * q + 4, :, :].bitcast(I32),
                 in_=hs_scales[:, 4 * q : 4 * q + 4, :].rearrange("a r n -> r a n").bitcast(I32),
             )
 
-        dn_raw, x_raw = [], []
-        for a in range(2):
-            dn_raw.append(load_pass(keep, "dn_raw%d" % a, "dn_raw%d" % a, dn, a))
-            x_raw.append(load_pass(wide, "x_raw%d" % a, "wide", x, a))
-        hs_codes = keep.tile([P, 2, R], U32, name="hs_codes", align_bytes=64)
-        nc.sync.dma_start(out=hs_codes[:].bitcast(I32), in_=hs_words.rearrange("a p r i -> p a (r i)").bitcast(I32))
-        dy_raw = [load_pass(wide, "dy0_raw%d" % a, "wide", dy0, a) for a in range(2)]
+        dy_raw = [load_pass(wide, "dy1_raw%d" % a, "wide", dy1, a) for a in range(2)]
 
         dn_q, x_q = [], []
         for a in range(2):
             dn_g = new_stage()
-            interleave(nc.scalar.copy, dn_g, dn_raw[a], 0, 0, SCALAR_COLS)
-            interleave(nc.vector.tensor_copy, dn_g, dn_raw[a], 0, SCALAR_COLS, COLS)
+            interleave(nc.scalar.copy, dn_g, dn_raw[:, a], 0, 0, SCALAR_COLS)
+            interleave(nc.vector.tensor_copy, dn_g, dn_raw[:, a], 0, SCALAR_COLS, COLS)
             dn_q.append(quantize("dn%d" % a, dn_g, E4M3))
             x_g0 = new_stage()
             interleave_permuted(nc.vector.tensor_copy, x_g0, x_raw[a], 0)
             x_g1 = new_stage()
             interleave_permuted(nc.scalar.copy, x_g1, x_raw[a], COLS)
             x_q.append([quantize("x%d0" % a, x_g0, E4M3), quantize("x%d1" % a, x_g1, E4M3)])
-            if a == 0:
-                dy_raw.append(load_pass(wide, "dy1_raw0", "wide", dy1, 0))
-        head_cols = N - COLS
-        dy_raw.append(load_pass(wide, "dy1_raw1", "wide", dy1[:, :head_cols], 1))
-        dy_last = load_pass(keep, "dy_last", "dy_last", dy1[:, head_cols:], 1)
+        dy_raw.append(load_pass(wide, "dy0_raw0", "wide", dy0, 0))
+        hs_codes = keep.tile([P, 2, R], U32, name="hs_codes", align_bytes=64)
+        nc.sync.dma_start(out=hs_codes[:].bitcast(I32), in_=hs_words.rearrange("a p r i -> p a (r i)").bitcast(I32))
+        dy_raw.append(load_pass(wide, "dy0_raw1", "wide", dy0[:, : N - COLS], 1))
+        dy_last = load_pass(keep, "dy_last", "dy_last", dy0[:, N - COLS :], 1)
 
         mom_sb = []
         for r in range(R_TILES):
@@ -113,7 +110,7 @@ def tile_mix_lorab_ema_kernel(tc, x, dn, hs_words, hs_scales, dy0, dy1, mom, out
             nc.sync.dma_start(out=m_tile[:], in_=mom[r * P : (r + 1) * P, :])
             mom_sb.append(m_tile)
 
-        lhs = [(hs_codes[:, a, :], hs_plane[:, a, :]) for a in range(2)]
+        lhs = []
         for b in range(2):
             h_g = new_stage()
             for r in range(R_TILES):
@@ -121,8 +118,11 @@ def tile_mix_lorab_ema_kernel(tc, x, dn, hs_words, hs_scales, dy0, dy1, mom, out
                 for s in range(PACK):
                     for a in range(2):
                         mx_pass(bank[:, s * P : (s + 1) * P], x_q[a][b], s * P, dn_q[a], r * P, P, E4M3, a == 0, a == 1)
-                nc.scalar.copy(out=h_g[:, r * P : (r + 1) * P, :], in_=bank[:].rearrange("p (s n) -> p n s", s=PACK))
+                copy = nc.scalar.copy if b == 0 else nc.vector.tensor_copy
+                copy(out=h_g[:, r * P : (r + 1) * P, :], in_=bank[:].rearrange("p (s n) -> p n s", s=PACK))
             lhs.append(quantize("h%d" % b, h_g, E4M3))
+
+        lhs.extend((hs_codes[:, a, :], hs_plane[:, a, :]) for a in range(2))
 
         tiles = [(r, c) for r in range(R_TILES) for c in range(N_CHUNKS)]
         early, late = tiles[:BANKS], tiles[BANKS:]

@@ -144,7 +144,8 @@ def tile_mix_lorab_ema_kernel(tc, x, dn, hs_words, hs_scales, dy0, dy1, mom, out
                 out=mom_sb[r][:, cols], in0=mom_sb[r][:, cols], scalar=0.9, in1=acc[rc][:], op0=ALU.mult, op1=ALU.add
             )
             if c == N_CHUNKS - 1:
-                nc.sync.dma_start(out=out[r * P : (r + 1) * P, :], in_=mom_sb[r][:])
+                queue = nc.sync if r % 2 == 0 else nc.scalar
+                queue.dma_start(out=out[r * P : (r + 1) * P, :], in_=mom_sb[r][:])
 
         for rc in early:
             open_tile(rc)

@@ -19,7 +19,8 @@ PACK = 4
 ROWS = P * PACK
 COLS = 512
 SCALAR_COLS = 256
-SCALAR_COLS_LAST = 176
+HALF = COLS // 2
+SCALAR_COLS_LAST = 192
 R_TILES = R // P
 N_CHUNKS = N // COLS
 BANKS = 8
@@ -99,9 +100,13 @@ def tile_mix_lorab_ema_kernel(tc, x, dn, hs_words, hs_scales, dy0, dy1, mom, out
             interleave_permuted(nc.scalar.copy, x_g1, x_raw[a], COLS)
             x_q.append([quantize("x%d0" % a, x_g0, E4M3), quantize("x%d1" % a, x_g1, E4M3)])
         dy_raw.append(load_pass(wide, "dy0_raw0", "wide", dy0, 0))
-        hs_codes = keep.tile([P, 2, R], U32, name="hs_codes", align_bytes=64)
-        nc.sync.dma_start(out=hs_codes[:].bitcast(I32), in_=hs_words.rearrange("a p r i -> p a (r i)").bitcast(I32))
-        dy_raw.append(load_pass(wide, "dy0_raw1", "wide", dy0[:, : N - COLS], 1))
+        hs_codes = []
+        for a in range(2):
+            if a == 1:
+                dy_raw.append(load_pass(wide, "dy0_raw1", "wide", dy0[:, : N - COLS], 1))
+            words = keep.tile([P, R], U32, name="hs_codes%d" % a, align_bytes=64)
+            nc.sync.dma_start(out=words[:].bitcast(I32), in_=hs_words[a].rearrange("p r i -> p (r i)").bitcast(I32))
+            hs_codes.append(words)
         dy_last = load_pass(keep, "dy_last", "dy_last", dy0[:, N - COLS :], 1)
 
         mom_sb = []
@@ -122,7 +127,7 @@ def tile_mix_lorab_ema_kernel(tc, x, dn, hs_words, hs_scales, dy0, dy1, mom, out
                 copy(out=h_g[:, r * P : (r + 1) * P, :], in_=bank[:].rearrange("p (s n) -> p n s", s=PACK))
             lhs.append(quantize("h%d" % b, h_g, E4M3))
 
-        lhs.extend((hs_codes[:, a, :], hs_plane[:, a, :]) for a in range(2))
+        lhs.extend((hs_codes[a], hs_plane[:, a, :]) for a in range(2))
 
         tiles = [(r, c) for r in range(R_TILES) for c in range(N_CHUNKS)]
         early, late = tiles[:BANKS], tiles[BANKS:]
@@ -151,7 +156,6 @@ def tile_mix_lorab_ema_kernel(tc, x, dn, hs_words, hs_scales, dy0, dy1, mom, out
             open_tile(rc)
         loads = [(g, dy_raw[g], range(N_CHUNKS), SCALAR_COLS) for g in range(3)]
         loads.append((3, dy_raw[3], range(N_CHUNKS - 1), SCALAR_COLS))
-        loads.append((3, dy_last, range(N_CHUNKS - 1, N_CHUNKS), SCALAR_COLS_LAST))
         for g, raw, chunks, split in loads:
             groups = {}
             for c in chunks:
@@ -165,6 +169,23 @@ def tile_mix_lorab_ema_kernel(tc, x, dn, hs_words, hs_scales, dy0, dy1, mom, out
                 for rc in early:
                     if rc[1] == c:
                         out_pass(rc, g)
+
+        halves = [stage.tile([P, HALF, PACK], BF16, name="half%d" % u, tag="grouped", align_bytes=64) for u in range(2)]
+        interleave(nc.scalar.copy, halves[1], dy_last, HALF, 0, SCALAR_COLS_LAST)
+        interleave(nc.vector.tensor_copy, halves[0], dy_last, 0, 0, HALF)
+        interleave(nc.vector.tensor_copy, halves[1], dy_last, HALF, SCALAR_COLS_LAST, HALF)
+        last_codes = keep.tile([P, COLS], U32, name="last_codes", align_bytes=64)
+        last_scales = keep.tile([P, COLS], U8, name="last_scales", align_bytes=64)
+        for u in range(2):
+            nc.vector.quantize_mx(
+                out=last_codes[:, u * HALF : (u + 1) * HALF].bitcast(E5M2),
+                scales=last_scales[:, u * HALF : (u + 1) * HALF],
+                in_=halves[u][:].rearrange("p c j -> p (c j)"),
+            )
+        dy_q[3, N_CHUNKS - 1] = (last_codes, last_scales)
+        for rc in early:
+            if rc[1] == N_CHUNKS - 1:
+                out_pass(rc, 3)
 
         for i, rc in enumerate(tiles):
             finish(rc)

@@ -24,6 +24,7 @@ SCALAR_COLS_LAST = 192
 R_TILES = R // P
 N_CHUNKS = N // COLS
 BANKS = 8
+DMA_ALIGN = 256
 
 
 def tile_mix_lorab_ema_kernel(tc, x, dn, hs_words, hs_scales, dy0, dy1, mom, out):
@@ -38,7 +39,7 @@ def tile_mix_lorab_ema_kernel(tc, x, dn, hs_words, hs_scales, dy0, dy1, mom, out
 
         def load_pass(pool, name, tag, src, a):
             width = src.shape[1]
-            raw = pool.tile([P, PACK, width], F32, name=name, tag=tag)
+            raw = pool.tile([P, PACK, width], F32, name=name, tag=tag, align_bytes=DMA_ALIGN)
             nc.sync.dma_start(out=raw[:], in_=src[a * ROWS : (a + 1) * ROWS, :].rearrange("(p j) w -> p j w", j=PACK))
             return raw
 
@@ -75,10 +76,10 @@ def tile_mix_lorab_ema_kernel(tc, x, dn, hs_words, hs_scales, dy0, dy1, mom, out
                 stop=stop,
             )
 
-        dn_raw = keep.tile([P, 2, PACK, R], F32, name="dn_raw")
+        dn_raw = keep.tile([P, 2, PACK, R], F32, name="dn_raw", align_bytes=DMA_ALIGN)
         nc.sync.dma_start(out=dn_raw[:], in_=dn.rearrange("(a p j) w -> p a j w", a=2, j=PACK))
         x_raw = [load_pass(wide, "x_raw%d" % a, "wide", x, a) for a in range(2)]
-        hs_plane = keep.tile([P, 2, R], U8, name="hs_plane", align_bytes=64)
+        hs_plane = keep.tile([P, 2, R], U8, name="hs_plane", align_bytes=DMA_ALIGN)
         nc.vector.memset(hs_plane[:].bitcast(I32), 0)
         for q in range(4):
             nc.scalar.dma_start(
@@ -104,14 +105,14 @@ def tile_mix_lorab_ema_kernel(tc, x, dn, hs_words, hs_scales, dy0, dy1, mom, out
         for a in range(2):
             if a == 1:
                 dy_raw.append(load_pass(wide, "dy0_raw1", "wide", dy0[:, : N - COLS], 1))
-            words = keep.tile([P, R], U32, name="hs_codes%d" % a, align_bytes=64)
+            words = keep.tile([P, R], U32, name="hs_codes%d" % a, align_bytes=DMA_ALIGN)
             nc.sync.dma_start(out=words[:].bitcast(I32), in_=hs_words[a].rearrange("p r i -> p (r i)").bitcast(I32))
             hs_codes.append(words)
         dy_last = load_pass(keep, "dy_last", "dy_last", dy0[:, N - COLS :], 1)
 
         mom_sb = []
         for r in range(R_TILES):
-            m_tile = keep.tile([P, N], F32, name="mom%d" % r)
+            m_tile = keep.tile([P, N], F32, name="mom%d" % r, align_bytes=DMA_ALIGN)
             nc.sync.dma_start(out=m_tile[:], in_=mom[r * P : (r + 1) * P, :])
             mom_sb.append(m_tile)
 

@@ -19,8 +19,7 @@ PACK = 4
 ROWS = P * PACK
 COLS = 512
 SCALAR_COLS = 256
-HALF = COLS // 2
-SCALAR_COLS_LAST = 192
+SCALAR_COLS_LAST = 384
 R_TILES = R // P
 N_CHUNKS = N // COLS
 BANKS = 8
@@ -32,7 +31,7 @@ def tile_mix_lorab_ema_kernel(tc, x, dn, hs_words, hs_scales, dy0, dy1, mom, out
 
     with ExitStack() as ctx:
         keep = ctx.enter_context(tc.tile_pool(name="keep", bufs=1))
-        wide = ctx.enter_context(tc.tile_pool(name="wide", bufs=4))
+        wide = ctx.enter_context(tc.tile_pool(name="wide", bufs=3))
         stage = ctx.enter_context(tc.tile_pool(name="stage", bufs=6))
         psum = ctx.enter_context(tc.psum_pool(name="psum", bufs=BANKS))
         ctx.enter_context(tc.manual_schedule())
@@ -104,11 +103,15 @@ def tile_mix_lorab_ema_kernel(tc, x, dn, hs_words, hs_scales, dy0, dy1, mom, out
         hs_codes = []
         for a in range(2):
             if a == 1:
-                dy_raw.append(load_pass(wide, "dy0_raw1", "wide", dy0[:, : N - COLS], 1))
+                pairs = []
+                for u in range(2):
+                    pair = keep.tile([P, 2, N], F32, name="pair%d" % u, align_bytes=DMA_ALIGN)
+                    rows = dy0[ROWS:, :].rearrange("(p j) w -> p j w", j=PACK)
+                    nc.sync.dma_start(out=pair[:], in_=rows[:, 2 * u : 2 * u + 2, :])
+                    pairs.append(pair)
             words = keep.tile([P, R], U32, name="hs_codes%d" % a, align_bytes=DMA_ALIGN)
             nc.sync.dma_start(out=words[:].bitcast(I32), in_=hs_words[a].rearrange("p r i -> p (r i)").bitcast(I32))
             hs_codes.append(words)
-        dy_last = load_pass(keep, "dy_last", "dy_last", dy0[:, N - COLS :], 1)
 
         mom_sb = []
         for r in range(R_TILES):
@@ -156,7 +159,6 @@ def tile_mix_lorab_ema_kernel(tc, x, dn, hs_words, hs_scales, dy0, dy1, mom, out
         for rc in early:
             open_tile(rc)
         loads = [(g, dy_raw[g], range(N_CHUNKS), SCALAR_COLS) for g in range(3)]
-        loads.append((3, dy_raw[3], range(N_CHUNKS - 1), SCALAR_COLS))
         for g, raw, chunks, split in loads:
             groups = {}
             for c in chunks:
@@ -171,25 +173,34 @@ def tile_mix_lorab_ema_kernel(tc, x, dn, hs_words, hs_scales, dy0, dy1, mom, out
                     if rc[1] == c:
                         out_pass(rc, g)
 
-        halves = [stage.tile([P, HALF, PACK], BF16, name="half%d" % u, tag="grouped", align_bytes=64) for u in range(2)]
-        interleave(nc.scalar.copy, halves[1], dy_last, HALF, 0, SCALAR_COLS_LAST)
-        interleave(nc.vector.tensor_copy, halves[0], dy_last, 0, 0, HALF)
-        interleave(nc.vector.tensor_copy, halves[1], dy_last, HALF, SCALAR_COLS_LAST, HALF)
-        last_codes = keep.tile([P, COLS], U32, name="last_codes", align_bytes=64)
-        last_scales = keep.tile([P, COLS], U8, name="last_scales", align_bytes=64)
-        for u in range(2):
-            nc.vector.quantize_mx(
-                out=last_codes[:, u * HALF : (u + 1) * HALF].bitcast(E5M2),
-                scales=last_scales[:, u * HALF : (u + 1) * HALF],
-                in_=halves[u][:].rearrange("p c j -> p (c j)"),
-            )
-        dy_q[3, N_CHUNKS - 1] = (last_codes, last_scales)
-        for rc in early:
-            if rc[1] == N_CHUNKS - 1:
-                out_pass(rc, 3)
+        groups = [new_stage() for c in range(N_CHUNKS)]
 
+        def interleave_pair(copy, u, c, lo, hi):
+            copy(
+                out=groups[c][:, lo:hi, 2 * u : 2 * u + 2].rearrange("p (c i) j -> p c j i", i=4),
+                in_=pairs[u][:, :, c * COLS + lo : c * COLS + hi].rearrange("p j (c i) -> p c j i", i=4),
+            )
+
+        interleave_pair(nc.vector.tensor_copy, 0, 0, 0, COLS)
+        interleave_pair(nc.scalar.copy, 0, 1, 0, COLS)
+        interleave_pair(nc.vector.tensor_copy, 0, 2, 0, COLS)
+
+        def close_chunk(c):
+            dy_q[3, c] = quantize("dy3%d" % c, groups[c], E5M2)
+            for rc in early:
+                if rc[1] == c:
+                    out_pass(rc, 3)
+
+        interleave_pair(nc.vector.tensor_copy, 1, 0, 0, COLS)
+        interleave_pair(nc.scalar.copy, 1, 1, 0, COLS)
+        interleave_pair(nc.scalar.copy, 1, 2, 0, SCALAR_COLS_LAST)
+        interleave_pair(nc.vector.tensor_copy, 1, 2, SCALAR_COLS_LAST, COLS)
+        close_chunk(0)
+        close_chunk(1)
         for i, rc in enumerate(tiles):
             finish(rc)
+            if i == 0:
+                close_chunk(2)
             if i < len(late):
                 open_tile(late[i])
                 for g in range(4):

@@ -100,17 +100,14 @@ def tile_mix_lorab_ema_kernel(tc, x, dn, hs_words, hs_scales, dy0, dy1, mom, out
             interleave_permuted(nc.scalar.copy, x_g1, x_raw[a], COLS)
             x_q.append([quantize("x%d0" % a, x_g0, E4M3), quantize("x%d1" % a, x_g1, E4M3)])
         dy_raw.append(load_pass(wide, "dy0_raw0", "wide", dy0, 0))
-        hs_codes = []
-        for a in range(2):
-            if a == 1:
-                pairs = []
-                for u in range(2):
-                    pair = keep.tile([P, 2, N], F32, name="pair%d" % u, align_bytes=DMA_ALIGN)
-                    rows = dy0[ROWS:, :].rearrange("(p j) w -> p j w", j=PACK)
-                    nc.sync.dma_start(out=pair[:], in_=rows[:, 2 * u : 2 * u + 2, :])
-                    pairs.append(pair)
-            words = keep.tile([P, R], U32, name="hs_codes%d" % a, align_bytes=DMA_ALIGN)
-            nc.sync.dma_start(out=words[:].bitcast(I32), in_=hs_words[a].rearrange("p r i -> p (r i)").bitcast(I32))
+        rows = dy0[ROWS:, :].rearrange("(p j) w -> p j w", j=PACK)
+        pairs, hs_codes = [], []
+        for u in range(2):
+            pair = keep.tile([P, 2, N], F32, name="pair%d" % u, align_bytes=DMA_ALIGN)
+            nc.sync.dma_start(out=pair[:], in_=rows[:, 2 * u : 2 * u + 2, :])
+            pairs.append(pair)
+            words = keep.tile([P, R], U32, name="hs_codes%d" % u, align_bytes=DMA_ALIGN)
+            nc.sync.dma_start(out=words[:].bitcast(I32), in_=hs_words[u].rearrange("p r i -> p (r i)").bitcast(I32))
             hs_codes.append(words)
 
         mom_sb = []

@@ -18,12 +18,16 @@ P = 128
 PACK = 4
 ROWS = P * PACK
 COLS = 512
-SCALAR_COLS = 256
-SCALAR_COLS_LAST = 384
 R_TILES = R // P
 N_CHUNKS = N // COLS
+LAST = N_CHUNKS - 1
 BANKS = 8
+MX_ALIGN = 64
 DMA_ALIGN = 256
+SCALAR_COLS = 256
+SCALAR_COLS_LAST = 192
+RAW_BUFS = 3
+STAGE_BUFS = 6
 
 
 def tile_mix_lorab_ema_kernel(tc, x, dn, hs_words, hs_scales, dy0, dy1, mom, out):
@@ -31,19 +35,18 @@ def tile_mix_lorab_ema_kernel(tc, x, dn, hs_words, hs_scales, dy0, dy1, mom, out
 
     with ExitStack() as ctx:
         keep = ctx.enter_context(tc.tile_pool(name="keep", bufs=1))
-        wide = ctx.enter_context(tc.tile_pool(name="wide", bufs=3))
-        stage = ctx.enter_context(tc.tile_pool(name="stage", bufs=6))
+        wide = ctx.enter_context(tc.tile_pool(name="wide", bufs=RAW_BUFS))
+        stage = ctx.enter_context(tc.tile_pool(name="stage", bufs=STAGE_BUFS))
         psum = ctx.enter_context(tc.psum_pool(name="psum", bufs=BANKS))
         ctx.enter_context(tc.manual_schedule())
 
-        def load_pass(pool, name, tag, src, a):
-            width = src.shape[1]
-            raw = pool.tile([P, PACK, width], F32, name=name, tag=tag, align_bytes=DMA_ALIGN)
+        def load_pass(name, src, a):
+            raw = wide.tile([P, PACK, src.shape[1]], F32, name=name, tag="wide", align_bytes=DMA_ALIGN)
             nc.sync.dma_start(out=raw[:], in_=src[a * ROWS : (a + 1) * ROWS, :].rearrange("(p j) w -> p j w", j=PACK))
             return raw
 
         def new_stage():
-            grouped = stage.tile([P, COLS, PACK], BF16, name="grouped", tag="grouped", align_bytes=64)
+            grouped = stage.tile([P, COLS, PACK], BF16, name="grouped", tag="grouped", align_bytes=MX_ALIGN)
             return grouped
 
         def interleave(copy, grouped, raw, first, lo, hi):
@@ -59,14 +62,14 @@ def tile_mix_lorab_ema_kernel(tc, x, dn, hs_words, hs_scales, dy0, dy1, mom, out
             )
 
         def quantize(name, grouped, fmt):
-            codes = keep.tile([P, COLS], U32, name=name + "_codes", align_bytes=64)
-            scales = keep.tile([P, COLS], U8, name=name + "_scales", align_bytes=64)
+            codes = keep.tile([P, COLS], U32, name=name + "_codes", align_bytes=MX_ALIGN)
+            scales = keep.tile([P, COLS], U8, name=name + "_scales", align_bytes=MX_ALIGN)
             nc.vector.quantize_mx(out=codes[:].bitcast(fmt), scales=scales[:], in_=grouped[:].rearrange("p c j -> p (c j)"))
             return codes, scales
 
-        def mx_pass(acc, stationary, m0, moving, n0, n, moving_fmt, start, stop):
+        def mx_pass(bank, stationary, m0, moving, n0, n, moving_fmt, start, stop):
             nc.tensor.matmul_mx(
-                out=acc,
+                out=bank,
                 lhsT=stationary[0][:, m0 : m0 + P].bitcast(E4M3),
                 lhsT_scale=stationary[1][:, m0 : m0 + P],
                 rhs=moving[0][:, n0 : n0 + n].bitcast(moving_fmt),
@@ -77,16 +80,17 @@ def tile_mix_lorab_ema_kernel(tc, x, dn, hs_words, hs_scales, dy0, dy1, mom, out
 
         dn_raw = keep.tile([P, 2, PACK, R], F32, name="dn_raw", align_bytes=DMA_ALIGN)
         nc.sync.dma_start(out=dn_raw[:], in_=dn.rearrange("(a p j) w -> p a j w", a=2, j=PACK))
-        x_raw = [load_pass(wide, "x_raw%d" % a, "wide", x, a) for a in range(2)]
-        hs_plane = keep.tile([P, 2, R], U8, name="hs_plane", align_bytes=DMA_ALIGN)
-        nc.vector.memset(hs_plane[:].bitcast(I32), 0)
+        x_raw = [load_pass("x_raw%d" % a, x, a) for a in range(2)]
+
+        hs_scale_sb = keep.tile([P, 2, R], U8, name="hs_plane", align_bytes=DMA_ALIGN)
+        nc.vector.memset(hs_scale_sb[:].bitcast(I32), 0)
         for q in range(4):
             nc.scalar.dma_start(
-                out=hs_plane[32 * q : 32 * q + 4, :, :].bitcast(I32),
+                out=hs_scale_sb[32 * q : 32 * q + 4, :, :].bitcast(I32),
                 in_=hs_scales[:, 4 * q : 4 * q + 4, :].rearrange("a r n -> r a n").bitcast(I32),
             )
 
-        dy_raw = [load_pass(wide, "dy1_raw%d" % a, "wide", dy1, a) for a in range(2)]
+        dy_raw = [load_pass("dy1_raw%d" % a, dy1, a) for a in range(2)]
 
         dn_q, x_q = [], []
         for a in range(2):
@@ -99,16 +103,20 @@ def tile_mix_lorab_ema_kernel(tc, x, dn, hs_words, hs_scales, dy0, dy1, mom, out
             x_g1 = new_stage()
             interleave_permuted(nc.scalar.copy, x_g1, x_raw[a], COLS)
             x_q.append([quantize("x%d0" % a, x_g0, E4M3), quantize("x%d1" % a, x_g1, E4M3)])
-        dy_raw.append(load_pass(wide, "dy0_raw0", "wide", dy0, 0))
+        dy_raw.append(load_pass("dy0_raw0", dy0, 0))
+
         rows = dy0[ROWS:, :].rearrange("(p j) w -> p j w", j=PACK)
         pairs, hs_codes = [], []
         for u in range(2):
-            pair = keep.tile([P, 2, N], F32, name="pair%d" % u, align_bytes=DMA_ALIGN)
-            nc.sync.dma_start(out=pair[:], in_=rows[:, 2 * u : 2 * u + 2, :])
+            width = N if u == 0 else N - COLS
+            pair = keep.tile([P, 2, width], F32, name="pair%d" % u, align_bytes=DMA_ALIGN)
+            nc.sync.dma_start(out=pair[:], in_=rows[:, 2 * u : 2 * u + 2, :width])
             pairs.append(pair)
             words = keep.tile([P, R], U32, name="hs_codes%d" % u, align_bytes=DMA_ALIGN)
             nc.sync.dma_start(out=words[:].bitcast(I32), in_=hs_words[u].rearrange("p r i -> p (r i)").bitcast(I32))
             hs_codes.append(words)
+        corner = keep.tile([P, 2, COLS], F32, name="corner", align_bytes=DMA_ALIGN)
+        nc.sync.dma_start(out=corner[:], in_=rows[:, 2:, N - COLS :])
 
         mom_sb = []
         for r in range(R_TILES):
@@ -128,7 +136,7 @@ def tile_mix_lorab_ema_kernel(tc, x, dn, hs_words, hs_scales, dy0, dy1, mom, out
                 copy(out=h_g[:, r * P : (r + 1) * P, :], in_=bank[:].rearrange("p (s n) -> p n s", s=PACK))
             lhs.append(quantize("h%d" % b, h_g, E4M3))
 
-        lhs.extend((hs_codes[a], hs_plane[:, a, :]) for a in range(2))
+        lhs.extend((hs_codes[a], hs_scale_sb[:, a, :]) for a in range(2))
 
         tiles = [(r, c) for r in range(R_TILES) for c in range(N_CHUNKS)]
         early, late = tiles[:BANKS], tiles[BANKS:]
@@ -149,55 +157,46 @@ def tile_mix_lorab_ema_kernel(tc, x, dn, hs_words, hs_scales, dy0, dy1, mom, out
             nc.vector.scalar_tensor_tensor(
                 out=mom_sb[r][:, cols], in0=mom_sb[r][:, cols], scalar=0.9, in1=acc[rc][:], op0=ALU.mult, op1=ALU.add
             )
-            if c == N_CHUNKS - 1:
+            if c == LAST:
                 queue = nc.sync if r % 2 == 0 else nc.scalar
                 queue.dma_start(out=out[r * P : (r + 1) * P, :], in_=mom_sb[r][:])
 
+        def close_chunk(g, c, grouped):
+            dy_q[g, c] = quantize("dy%d%d" % (g, c), grouped, E5M2)
+            for rc in early:
+                if rc[1] == c:
+                    out_pass(rc, g)
+
         for rc in early:
             open_tile(rc)
-        loads = [(g, dy_raw[g], range(N_CHUNKS), SCALAR_COLS) for g in range(3)]
-        for g, raw, chunks, split in loads:
-            groups = {}
-            for c in chunks:
+        for g in range(3):
+            groups = []
+            for c in range(N_CHUNKS):
                 dy_g = new_stage()
-                first = (c - chunks.start) * COLS
-                interleave(nc.scalar.copy, dy_g, raw, first, 0, split)
-                interleave(nc.vector.tensor_copy, dy_g, raw, first, split, COLS)
-                groups[c] = dy_g
-            for c in chunks:
-                dy_q[g, c] = quantize("dy%d%d" % (g, c), groups[c], E5M2)
-                for rc in early:
-                    if rc[1] == c:
-                        out_pass(rc, g)
+                interleave(nc.scalar.copy, dy_g, dy_raw[g], c * COLS, 0, SCALAR_COLS)
+                interleave(nc.vector.tensor_copy, dy_g, dy_raw[g], c * COLS, SCALAR_COLS, COLS)
+                groups.append(dy_g)
+            for c in range(N_CHUNKS):
+                close_chunk(g, c, groups[c])
 
         groups = [new_stage() for c in range(N_CHUNKS)]
 
-        def interleave_pair(copy, u, c, lo, hi):
-            copy(
-                out=groups[c][:, lo:hi, 2 * u : 2 * u + 2].rearrange("p (c i) j -> p c j i", i=4),
-                in_=pairs[u][:, :, c * COLS + lo : c * COLS + hi].rearrange("p j (c i) -> p c j i", i=4),
-            )
+        def interleave_pair(copy, u, c, raw, first, lo, hi):
+            interleave(copy, groups[c][:, :, 2 * u : 2 * u + 2], raw, first, lo, hi)
 
-        interleave_pair(nc.vector.tensor_copy, 0, 0, 0, COLS)
-        interleave_pair(nc.scalar.copy, 0, 1, 0, COLS)
-        interleave_pair(nc.vector.tensor_copy, 0, 2, 0, COLS)
+        interleave_pair(nc.vector.tensor_copy, 0, 0, pairs[0], 0, 0, COLS)
+        interleave_pair(nc.scalar.copy, 0, 1, pairs[0], COLS, 0, COLS)
+        interleave_pair(nc.vector.tensor_copy, 0, LAST, pairs[0], LAST * COLS, 0, COLS)
+        interleave_pair(nc.vector.tensor_copy, 1, 0, pairs[1], 0, 0, COLS)
+        interleave_pair(nc.scalar.copy, 1, 1, pairs[1], COLS, 0, COLS)
+        interleave_pair(nc.scalar.copy, 1, LAST, corner, 0, 0, SCALAR_COLS_LAST)
+        close_chunk(3, 0, groups[0])
+        interleave_pair(nc.vector.tensor_copy, 1, LAST, corner, 0, SCALAR_COLS_LAST, COLS)
+        close_chunk(3, 1, groups[1])
+        close_chunk(3, LAST, groups[LAST])
 
-        def close_chunk(c):
-            dy_q[3, c] = quantize("dy3%d" % c, groups[c], E5M2)
-            for rc in early:
-                if rc[1] == c:
-                    out_pass(rc, 3)
-
-        interleave_pair(nc.vector.tensor_copy, 1, 0, 0, COLS)
-        interleave_pair(nc.scalar.copy, 1, 1, 0, COLS)
-        interleave_pair(nc.scalar.copy, 1, 2, 0, SCALAR_COLS_LAST)
-        interleave_pair(nc.vector.tensor_copy, 1, 2, SCALAR_COLS_LAST, COLS)
-        close_chunk(0)
-        close_chunk(1)
         for i, rc in enumerate(tiles):
             finish(rc)
-            if i == 0:
-                close_chunk(2)
             if i < len(late):
                 open_tile(late[i])
                 for g in range(4):

@@ -84,10 +84,10 @@ def tile_mix_lorab_ema_kernel(tc, x, dn, hs_words, hs_scales, dy0, dy1, mom, out
 
         hs_scale_sb = keep.tile([P, 2, R], U8, name="hs_plane", align_bytes=DMA_ALIGN)
         nc.vector.memset(hs_scale_sb[:].bitcast(I32), 0)
-        for q in range(4):
+        for i in range(4):
             nc.scalar.dma_start(
-                out=hs_scale_sb[32 * q : 32 * q + 4, :, :].bitcast(I32),
-                in_=hs_scales[:, 4 * q : 4 * q + 4, :].rearrange("a r n -> r a n").bitcast(I32),
+                out=hs_scale_sb[i:P:32, :, :].bitcast(I32),
+                in_=hs_scales.rearrange("a (q i) n -> i q a n", i=4)[i].bitcast(I32),
             )
 
         dy_raw = [load_pass("dy1_raw%d" % a, dy1, a) for a in range(2)]

@@ -37,7 +37,7 @@ def tile_mix_lorab_ema_kernel(tc, x, dn, hs_words, hs_scales, dy0, dy1, mom, out
         keep = ctx.enter_context(tc.tile_pool(name="keep", bufs=1))
         wide = ctx.enter_context(tc.tile_pool(name="wide", bufs=RAW_BUFS))
         stage = ctx.enter_context(tc.tile_pool(name="stage", bufs=STAGE_BUFS))
-        psum = ctx.enter_context(tc.psum_pool(name="psum", bufs=BANKS))
+        psum = ctx.enter_context(tc.psum_pool(name="psum", bufs=1))
         ctx.enter_context(tc.manual_schedule())
 
         def load_pass(name, src, a):
@@ -105,18 +105,20 @@ def tile_mix_lorab_ema_kernel(tc, x, dn, hs_words, hs_scales, dy0, dy1, mom, out
             x_q.append([quantize("x%d0" % a, x_g0, E4M3), quantize("x%d1" % a, x_g1, E4M3)])
         dy_raw.append(load_pass("dy0_raw0", dy0, 0))
 
-        rows = dy0[ROWS:, :].rearrange("(p j) w -> p j w", j=PACK)
-        pairs, hs_codes = [], []
-        for u in range(2):
-            width = N if u == 0 else N - COLS
-            pair = keep.tile([P, 2, width], F32, name="pair%d" % u, align_bytes=DMA_ALIGN)
-            nc.sync.dma_start(out=pair[:], in_=rows[:, 2 * u : 2 * u + 2, :width])
-            pairs.append(pair)
-            words = keep.tile([P, R], U32, name="hs_codes%d" % u, align_bytes=DMA_ALIGN)
-            nc.sync.dma_start(out=words[:].bitcast(I32), in_=hs_words[u].rearrange("p r i -> p (r i)").bitcast(I32))
-            hs_codes.append(words)
-        corner = keep.tile([P, 2, COLS], F32, name="corner", align_bytes=DMA_ALIGN)
-        nc.sync.dma_start(out=corner[:], in_=rows[:, 2:, N - COLS :])
+        run = dy0[ROWS:, :].rearrange("(p j) w -> p (j w)", j=PACK)
+        pairs = [keep.tile([P, 2, N], F32, name="pair%d" % u, align_bytes=DMA_ALIGN) for u in range(2)]
+        hs_codes = [keep.tile([P, R], U32, name="hs_codes%d" % a, align_bytes=DMA_ALIGN) for a in range(2)]
+
+        def load_hs(a):
+            nc.sync.dma_start(
+                out=hs_codes[a][:].bitcast(I32), in_=hs_words[a].rearrange("p r i -> p (r i)").bitcast(I32)
+            )
+
+        nc.sync.dma_start(out=pairs[0][:].rearrange("p j w -> p (j w)"), in_=run[:, : 2 * N])
+        load_hs(0)
+        nc.sync.dma_start(out=pairs[1][:].rearrange("p j w -> p (j w)")[:, : N + COLS], in_=run[:, 2 * N : 3 * N + COLS])
+        nc.sync.dma_start(out=pairs[1][:, 1, COLS:], in_=run[:, 3 * N + COLS :])
+        load_hs(1)
 
         mom_sb = []
         for r in range(R_TILES):
@@ -128,7 +130,7 @@ def tile_mix_lorab_ema_kernel(tc, x, dn, hs_words, hs_scales, dy0, dy1, mom, out
         for b in range(2):
             h_g = new_stage()
             for r in range(R_TILES):
-                bank = psum.tile([P, COLS], F32, name="h_bank", tag="bank")
+                bank = psum.tile([P, COLS], F32, name="h_bank", tag="bank%d" % (R_TILES * b + r))
                 for s in range(PACK):
                     for a in range(2):
                         mx_pass(bank[:, s * P : (s + 1) * P], x_q[a][b], s * P, dn_q[a], r * P, P, E4M3, a == 0, a == 1)
@@ -143,8 +145,8 @@ def tile_mix_lorab_ema_kernel(tc, x, dn, hs_words, hs_scales, dy0, dy1, mom, out
         acc = {}
         dy_q = {}
 
-        def open_tile(rc):
-            bank = psum.tile([P, COLS], F32, name="acc", tag="bank")
+        def open_tile(rc, i):
+            bank = psum.tile([P, COLS], F32, name="acc", tag="bank%d" % i)
             acc[rc] = bank
 
         def out_pass(rc, g):
@@ -157,9 +159,11 @@ def tile_mix_lorab_ema_kernel(tc, x, dn, hs_words, hs_scales, dy0, dy1, mom, out
             nc.vector.scalar_tensor_tensor(
                 out=mom_sb[r][:, cols], in0=mom_sb[r][:, cols], scalar=0.9, in1=acc[rc][:], op0=ALU.mult, op1=ALU.add
             )
-            if c == LAST:
-                queue = nc.sync if r % 2 == 0 else nc.scalar
-                queue.dma_start(out=out[r * P : (r + 1) * P, :], in_=mom_sb[r][:])
+
+        def run_late(rc, freed):
+            open_tile(rc, early.index(freed))
+            for g in range(4):
+                out_pass(rc, g)
 
         def close_chunk(g, c, grouped):
             dy_q[g, c] = quantize("dy%d%d" % (g, c), grouped, E5M2)
@@ -167,8 +171,8 @@ def tile_mix_lorab_ema_kernel(tc, x, dn, hs_words, hs_scales, dy0, dy1, mom, out
                 if rc[1] == c:
                     out_pass(rc, g)
 
-        for rc in early:
-            open_tile(rc)
+        for i, rc in enumerate(early):
+            open_tile(rc, i)
         for g in range(3):
             groups = []
             for c in range(N_CHUNKS):
@@ -181,23 +185,35 @@ def tile_mix_lorab_ema_kernel(tc, x, dn, hs_words, hs_scales, dy0, dy1, mom, out
 
         groups = [new_stage() for c in range(N_CHUNKS)]
 
-        def interleave_pair(copy, u, c, raw, first, lo, hi):
-            interleave(copy, groups[c][:, :, 2 * u : 2 * u + 2], raw, first, lo, hi)
+        def interleave_pair(copy, u, c, lo, hi):
+            interleave(copy, groups[c][:, :, 2 * u : 2 * u + 2], pairs[u], c * COLS, lo, hi)
 
-        interleave_pair(nc.vector.tensor_copy, 0, 0, pairs[0], 0, 0, COLS)
-        interleave_pair(nc.scalar.copy, 0, 1, pairs[0], COLS, 0, COLS)
-        interleave_pair(nc.vector.tensor_copy, 0, LAST, pairs[0], LAST * COLS, 0, COLS)
-        interleave_pair(nc.vector.tensor_copy, 1, 0, pairs[1], 0, 0, COLS)
-        interleave_pair(nc.scalar.copy, 1, 1, pairs[1], COLS, 0, COLS)
-        interleave_pair(nc.scalar.copy, 1, LAST, corner, 0, 0, SCALAR_COLS_LAST)
+        interleave_pair(nc.vector.tensor_copy, 0, 0, 0, COLS)
+        interleave_pair(nc.scalar.copy, 0, 1, 0, COLS)
+        interleave_pair(nc.vector.tensor_copy, 0, LAST, 0, COLS)
+        interleave_pair(nc.scalar.copy, 1, 0, 0, SCALAR_COLS_LAST)
+        interleave_pair(nc.vector.tensor_copy, 1, 0, SCALAR_COLS_LAST, COLS)
         close_chunk(3, 0, groups[0])
-        interleave_pair(nc.vector.tensor_copy, 1, LAST, corner, 0, SCALAR_COLS_LAST, COLS)
+        interleave_pair(nc.vector.tensor_copy, 1, 1, 0, COLS)
+        interleave_pair(nc.scalar.copy, 1, LAST, 0, COLS)
         close_chunk(3, 1, groups[1])
         close_chunk(3, LAST, groups[LAST])
 
-        for i, rc in enumerate(tiles):
-            finish(rc)
-            if i < len(late):
-                open_tile(late[i])
-                for g in range(4):
-                    out_pass(late[i], g)
+        helped = [(1, 0), (2, 0)]
+        waiting = list(late)
+        sums = {}
+        for rc in helped:
+            sums[rc] = keep.tile([P, COLS], F32, name="sum%d" % rc[0])
+            nc.scalar.copy(out=sums[rc][:], in_=acc[rc][:])
+            run_late(waiting.pop(0), rc)
+        for r in range(R_TILES):
+            for c in range(N_CHUNKS):
+                if (r, c) in helped:
+                    part = mom_sb[r][:, :COLS]
+                    nc.scalar.mul(out=part, in_=part, mul=0.9)
+                    nc.gpsimd.tensor_tensor(out=part, in0=part, in1=sums[r, c][:], op=ALU.add)
+                else:
+                    finish((r, c))
+                if waiting:
+                    run_late(waiting.pop(0), (r, c))
+            nc.sync.dma_start(out=out[r * P : (r + 1) * P, :], in_=mom_sb[r][:])

@@ -26,6 +26,8 @@ MX_ALIGN = 64
 DMA_ALIGN = 256
 SCALAR_COLS = 256
 SCALAR_COLS_LAST = 192
+SCALAR_COLS_END = {1: 128, 2: 384}
+HELPED_COLS = 256
 RAW_BUFS = 3
 STAGE_BUFS = 6
 
@@ -153,11 +155,11 @@ def tile_mix_lorab_ema_kernel(tc, x, dn, hs_words, hs_scales, dy0, dy1, mom, out
             r, c = rc
             mx_pass(acc[rc][:], lhs[g], r * P, dy_q[g, c], 0, COLS, E5M2, g == 0, g == 3)
 
-        def finish(rc):
+        def finish(rc, lo):
             r, c = rc
-            cols = slice(c * COLS, (c + 1) * COLS)
+            part = mom_sb[r][:, c * COLS + lo : (c + 1) * COLS]
             nc.vector.scalar_tensor_tensor(
-                out=mom_sb[r][:, cols], in0=mom_sb[r][:, cols], scalar=0.9, in1=acc[rc][:], op0=ALU.mult, op1=ALU.add
+                out=part, in0=part, scalar=0.9, in1=acc[rc][:, lo:], op0=ALU.mult, op1=ALU.add
             )
 
         def run_late(rc, freed):
@@ -194,26 +196,21 @@ def tile_mix_lorab_ema_kernel(tc, x, dn, hs_words, hs_scales, dy0, dy1, mom, out
         interleave_pair(nc.scalar.copy, 1, 0, 0, SCALAR_COLS_LAST)
         interleave_pair(nc.vector.tensor_copy, 1, 0, SCALAR_COLS_LAST, COLS)
         close_chunk(3, 0, groups[0])
-        interleave_pair(nc.vector.tensor_copy, 1, 1, 0, COLS)
-        interleave_pair(nc.scalar.copy, 1, LAST, 0, COLS)
-        close_chunk(3, 1, groups[1])
-        close_chunk(3, LAST, groups[LAST])
+        for c in range(1, N_CHUNKS):
+            interleave_pair(nc.scalar.copy, 1, c, 0, SCALAR_COLS_END[c])
+            interleave_pair(nc.vector.tensor_copy, 1, c, SCALAR_COLS_END[c], COLS)
+        for c in range(1, N_CHUNKS):
+            close_chunk(3, c, groups[c])
 
-        helped = [(1, 0), (2, 0)]
         waiting = list(late)
-        sums = {}
-        for rc in helped:
-            sums[rc] = keep.tile([P, COLS], F32, name="sum%d" % rc[0])
-            nc.scalar.copy(out=sums[rc][:], in_=acc[rc][:])
-            run_late(waiting.pop(0), rc)
         for r in range(R_TILES):
+            sums = keep.tile([P, HELPED_COLS], F32, name="sums%d" % r)
+            nc.scalar.copy(out=sums[:], in_=acc[r, 0][:, :HELPED_COLS])
+            helped = mom_sb[r][:, :HELPED_COLS]
+            nc.scalar.mul(out=helped, in_=helped, mul=0.9)
+            nc.gpsimd.tensor_tensor(out=helped, in0=helped, in1=sums[:], op=ALU.add)
             for c in range(N_CHUNKS):
-                if (r, c) in helped:
-                    part = mom_sb[r][:, :COLS]
-                    nc.scalar.mul(out=part, in_=part, mul=0.9)
-                    nc.gpsimd.tensor_tensor(out=part, in0=part, in1=sums[r, c][:], op=ALU.add)
-                else:
-                    finish((r, c))
+                finish((r, c), HELPED_COLS if c == 0 else 0)
                 if waiting:
                     run_late(waiting.pop(0), (r, c))
             nc.sync.dma_start(out=out[r * P : (r + 1) * P, :], in_=mom_sb[r][:])

@@ -25,9 +25,7 @@ BANKS = 8
 MX_ALIGN = 64
 DMA_ALIGN = 256
 SCALAR_COLS = 256
-SCALAR_COLS_LAST = 192
-SCALAR_COLS_END = {1: 128, 2: 384}
-HELPED_COLS = 256
+SCALAR_COLS_LAST = (192, 128, 384)
 RAW_BUFS = 3
 STAGE_BUFS = 6
 
@@ -155,12 +153,10 @@ def tile_mix_lorab_ema_kernel(tc, x, dn, hs_words, hs_scales, dy0, dy1, mom, out
             r, c = rc
             mx_pass(acc[rc][:], lhs[g], r * P, dy_q[g, c], 0, COLS, E5M2, g == 0, g == 3)
 
-        def finish(rc, lo):
+        def finish(rc):
             r, c = rc
-            part = mom_sb[r][:, c * COLS + lo : (c + 1) * COLS]
-            nc.vector.scalar_tensor_tensor(
-                out=part, in0=part, scalar=0.9, in1=acc[rc][:, lo:], op0=ALU.mult, op1=ALU.add
-            )
+            part = mom_sb[r][:, c * COLS : (c + 1) * COLS]
+            nc.vector.scalar_tensor_tensor(out=part, in0=part, scalar=0.9, in1=acc[rc][:], op0=ALU.mult, op1=ALU.add)
 
         def run_late(rc, freed):
             open_tile(rc, early.index(freed))
@@ -193,24 +189,17 @@ def tile_mix_lorab_ema_kernel(tc, x, dn, hs_words, hs_scales, dy0, dy1, mom, out
         interleave_pair(nc.vector.tensor_copy, 0, 0, 0, COLS)
         interleave_pair(nc.scalar.copy, 0, 1, 0, COLS)
         interleave_pair(nc.vector.tensor_copy, 0, LAST, 0, COLS)
-        interleave_pair(nc.scalar.copy, 1, 0, 0, SCALAR_COLS_LAST)
-        interleave_pair(nc.vector.tensor_copy, 1, 0, SCALAR_COLS_LAST, COLS)
-        close_chunk(3, 0, groups[0])
-        for c in range(1, N_CHUNKS):
-            interleave_pair(nc.scalar.copy, 1, c, 0, SCALAR_COLS_END[c])
-            interleave_pair(nc.vector.tensor_copy, 1, c, SCALAR_COLS_END[c], COLS)
-        for c in range(1, N_CHUNKS):
-            close_chunk(3, c, groups[c])
+        for chunks in ([0], range(1, N_CHUNKS)):
+            for c in chunks:
+                interleave_pair(nc.scalar.copy, 1, c, 0, SCALAR_COLS_LAST[c])
+                interleave_pair(nc.vector.tensor_copy, 1, c, SCALAR_COLS_LAST[c], COLS)
+            for c in chunks:
+                close_chunk(3, c, groups[c])
 
         waiting = list(late)
         for r in range(R_TILES):
-            sums = keep.tile([P, HELPED_COLS], F32, name="sums%d" % r)
-            nc.scalar.copy(out=sums[:], in_=acc[r, 0][:, :HELPED_COLS])
-            helped = mom_sb[r][:, :HELPED_COLS]
-            nc.scalar.mul(out=helped, in_=helped, mul=0.9)
-            nc.gpsimd.tensor_tensor(out=helped, in0=helped, in1=sums[:], op=ALU.add)
             for c in range(N_CHUNKS):
-                finish((r, c), HELPED_COLS if c == 0 else 0)
+                finish((r, c))
                 if waiting:
                     run_late(waiting.pop(0), (r, c))
             nc.sync.dma_start(out=out[r * P : (r + 1) * P, :], in_=mom_sb[r][:])

@@ -85,7 +85,7 @@ def tile_mix_lorab_ema_kernel(tc, x, dn, hs_words, hs_scales, dy0, dy1, mom, out
         hs_scale_sb = keep.tile([P, 2, R], U8, name="hs_plane", align_bytes=DMA_ALIGN)
         nc.vector.memset(hs_scale_sb[:].bitcast(I32), 0)
         for i in range(4):
-            nc.scalar.dma_start(
+            nc.sync.dma_start(
                 out=hs_scale_sb[i:P:32, :, :].bitcast(I32),
                 in_=hs_scales.rearrange("a (q i) n -> i q a n", i=4)[i].bitcast(I32),
             )

@@ -80,17 +80,24 @@ def tile_mix_lorab_ema_kernel(tc, x, dn, hs_words, hs_scales, dy0, dy1, mom, out
 
         dn_raw = keep.tile([P, 2, PACK, R], F32, name="dn_raw", align_bytes=DMA_ALIGN)
         nc.sync.dma_start(out=dn_raw[:], in_=dn.rearrange("(a p j) w -> p a j w", a=2, j=PACK))
-        x_raw = [load_pass("x_raw%d" % a, x, a) for a in range(2)]
 
         hs_scale_sb = keep.tile([P, 2, R], U8, name="hs_plane", align_bytes=DMA_ALIGN)
         nc.vector.memset(hs_scale_sb[:].bitcast(I32), 0)
-        for i in range(4):
+
+        def load_scale_rows(i):
             nc.sync.dma_start(
                 out=hs_scale_sb[i:P:32, :, :].bitcast(I32),
                 in_=hs_scales.rearrange("a (q i) n -> i q a n", i=4)[i].bitcast(I32),
             )
 
-        dy_raw = [load_pass("dy1_raw%d" % a, dy1, a) for a in range(2)]
+        x_raw = []
+        for a in range(2):
+            x_raw.append(load_pass("x_raw%d" % a, x, a))
+            load_scale_rows(a)
+        dy_raw = []
+        for a in range(2):
+            dy_raw.append(load_pass("dy1_raw%d" % a, dy1, a))
+            load_scale_rows(2 + a)
 
         dn_q, x_q = [], []
         for a in range(2):

@@ -26,7 +26,6 @@ MX_ALIGN = 64
 DMA_ALIGN = 256
 SCALAR_COLS = 256
 SCALAR_COLS_LAST = (192, 128, 384)
-RAW_BUFS = 3
 STAGE_BUFS = 6
 
 
@@ -35,14 +34,13 @@ def tile_mix_lorab_ema_kernel(tc, x, dn, hs_words, hs_scales, dy0, dy1, mom, out
 
     with ExitStack() as ctx:
         keep = ctx.enter_context(tc.tile_pool(name="keep", bufs=1))
-        wide = ctx.enter_context(tc.tile_pool(name="wide", bufs=RAW_BUFS))
         stage = ctx.enter_context(tc.tile_pool(name="stage", bufs=STAGE_BUFS))
         psum = ctx.enter_context(tc.psum_pool(name="psum", bufs=1))
         ctx.enter_context(tc.manual_schedule())
 
-        def load_pass(name, src, a):
-            raw = wide.tile([P, PACK, src.shape[1]], F32, name=name, tag="wide", align_bytes=DMA_ALIGN)
-            nc.sync.dma_start(out=raw[:], in_=src[a * ROWS : (a + 1) * ROWS, :].rearrange("(p j) w -> p j w", j=PACK))
+        def load_passes(name, src, passes, tag):
+            raw = keep.tile([P, passes, PACK, src.shape[1]], F32, name=name, tag=tag, align_bytes=DMA_ALIGN)
+            nc.sync.dma_start(out=raw[:], in_=src[: passes * ROWS, :].rearrange("(a p j) w -> p a j w", a=passes, j=PACK))
             return raw
 
         def new_stage():
@@ -78,39 +76,32 @@ def tile_mix_lorab_ema_kernel(tc, x, dn, hs_words, hs_scales, dy0, dy1, mom, out
                 stop=stop,
             )
 
-        dn_raw = keep.tile([P, 2, PACK, R], F32, name="dn_raw", align_bytes=DMA_ALIGN)
-        nc.sync.dma_start(out=dn_raw[:], in_=dn.rearrange("(a p j) w -> p a j w", a=2, j=PACK))
+        dn_raw = [load_passes("dn_raw%d" % a, dn[a * ROWS :, :], 1, "dn_raw%d" % a)[:, 0] for a in range(2)]
+        x_raw = load_passes("x_raw", x, 2, "x_raw")
 
         hs_scale_sb = keep.tile([P, 2, R], U8, name="hs_plane", align_bytes=DMA_ALIGN)
         nc.vector.memset(hs_scale_sb[:].bitcast(I32), 0)
-
-        def load_scale_rows(i):
+        for i in range(4):
             nc.sync.dma_start(
                 out=hs_scale_sb[i:P:32, :, :].bitcast(I32),
                 in_=hs_scales.rearrange("a (q i) n -> i q a n", i=4)[i].bitcast(I32),
             )
+        dy_raw = [load_passes("dy1_raw%d" % a, dy1[a * ROWS :, :], 1, "dy1_raw%d" % a)[:, 0] for a in range(2)]
 
-        x_raw = []
-        for a in range(2):
-            x_raw.append(load_pass("x_raw%d" % a, x, a))
-            load_scale_rows(a)
-        dy_raw = []
-        for a in range(2):
-            dy_raw.append(load_pass("dy1_raw%d" % a, dy1, a))
-            load_scale_rows(2 + a)
-
-        dn_q, x_q = [], []
+        dn_q = []
         for a in range(2):
             dn_g = new_stage()
-            interleave(nc.scalar.copy, dn_g, dn_raw[:, a], 0, 0, SCALAR_COLS)
-            interleave(nc.vector.tensor_copy, dn_g, dn_raw[:, a], 0, SCALAR_COLS, COLS)
+            interleave(nc.scalar.copy, dn_g, dn_raw[a], 0, 0, SCALAR_COLS)
+            interleave(nc.vector.tensor_copy, dn_g, dn_raw[a], 0, SCALAR_COLS, COLS)
             dn_q.append(quantize("dn%d" % a, dn_g, E4M3))
-            x_g0 = new_stage()
-            interleave_permuted(nc.vector.tensor_copy, x_g0, x_raw[a], 0)
-            x_g1 = new_stage()
-            interleave_permuted(nc.scalar.copy, x_g1, x_raw[a], COLS)
-            x_q.append([quantize("x%d0" % a, x_g0, E4M3), quantize("x%d1" % a, x_g1, E4M3)])
-        dy_raw.append(load_pass("dy0_raw0", dy0, 0))
+        x_q = [[], []]
+        for b in range(2):
+            x_g = [new_stage() for a in range(2)]
+            interleave_permuted(nc.vector.tensor_copy, x_g[0], x_raw[:, 0], b * COLS)
+            interleave_permuted(nc.scalar.copy, x_g[1], x_raw[:, 1], b * COLS)
+            for a in range(2):
+                x_q[a].append(quantize("x%d%d" % (a, b), x_g[a], E4M3))
+        dy_raw.append(load_passes("dy0_raw", dy0, 1, "x_raw")[:, 0])
 
         run = dy0[ROWS:, :].rearrange("(p j) w -> p (j w)", j=PACK)
         pairs = [keep.tile([P, 2, N], F32, name="pair%d" % u, align_bytes=DMA_ALIGN) for u in range(2)]
@@ -209,4 +200,4 @@ def tile_mix_lorab_ema_kernel(tc, x, dn, hs_words, hs_scales, dy0, dy1, mom, out
                 finish((r, c))
                 if waiting:
                     run_late(waiting.pop(0), (r, c))
-            nc.sync.dma_start(out=out[r * P : (r + 1) * P, :], in_=mom_sb[r][:])
+            nc.scalar.dma_start(out=out[r * P : (r + 1) * P, :], in_=mom_sb[r][:])

@@ -26,7 +26,7 @@ MX_ALIGN = 64
 DMA_ALIGN = 256
 SCALAR_COLS = 256
 SCALAR_COLS_LAST = (192, 128, 384)
-STAGE_BUFS = 6
+STAGE_BUFS = 7
 
 
 def tile_mix_lorab_ema_kernel(tc, x, dn, hs_words, hs_scales, dy0, dy1, mom, out):
@@ -77,7 +77,7 @@ def tile_mix_lorab_ema_kernel(tc, x, dn, hs_words, hs_scales, dy0, dy1, mom, out
             )
 
         dn_raw = [load_passes("dn_raw%d" % a, dn[a * ROWS :, :], 1, "dn_raw%d" % a)[:, 0] for a in range(2)]
-        x_raw = load_passes("x_raw", x, 2, "x_raw")
+        x_raw = [load_passes("x_raw%d" % a, x[a * ROWS :, :], 1, "x_raw%d" % a)[:, 0] for a in range(2)]
 
         hs_scale_sb = keep.tile([P, 2, R], U8, name="hs_plane", align_bytes=DMA_ALIGN)
         nc.vector.memset(hs_scale_sb[:].bitcast(I32), 0)
@@ -94,17 +94,17 @@ def tile_mix_lorab_ema_kernel(tc, x, dn, hs_words, hs_scales, dy0, dy1, mom, out
             interleave(nc.scalar.copy, dn_g, dn_raw[a], 0, 0, SCALAR_COLS)
             interleave(nc.vector.tensor_copy, dn_g, dn_raw[a], 0, SCALAR_COLS, COLS)
             dn_q.append(quantize("dn%d" % a, dn_g, E4M3))
-        x_q = [[], []]
-        for b in range(2):
-            x_g = [new_stage() for a in range(2)]
-            interleave_permuted(nc.vector.tensor_copy, x_g[0], x_raw[:, 0], b * COLS)
-            interleave_permuted(nc.scalar.copy, x_g[1], x_raw[:, 1], b * COLS)
-            for a in range(2):
-                x_q[a].append(quantize("x%d%d" % (a, b), x_g[a], E4M3))
-        dy_raw.append(load_passes("dy0_raw", dy0, 1, "x_raw")[:, 0])
+        x_q = []
+        for a in range(2):
+            x_g = [new_stage() for b in range(2)]
+            interleave_permuted(nc.vector.tensor_copy, x_g[0], x_raw[a], 0)
+            interleave_permuted(nc.scalar.copy, x_g[1], x_raw[a], COLS)
+            x_q.append([quantize("x%d%d" % (a, b), x_g[b], E4M3) for b in range(2)])
+        dy_raw.append(load_passes("dy0_raw", dy0, 1, "x_raw0")[:, 0])
 
         run = dy0[ROWS:, :].rearrange("(p j) w -> p (j w)", j=PACK)
-        pairs = [keep.tile([P, 2, N], F32, name="pair%d" % u, align_bytes=DMA_ALIGN) for u in range(2)]
+        last_raw = keep.tile([P, PACK, N], F32, name="last_raw", align_bytes=DMA_ALIGN)
+        cut = 3 * N + COLS
         hs_codes = [keep.tile([P, R], U32, name="hs_codes%d" % a, align_bytes=DMA_ALIGN) for a in range(2)]
 
         def load_hs(a):
@@ -112,10 +112,9 @@ def tile_mix_lorab_ema_kernel(tc, x, dn, hs_words, hs_scales, dy0, dy1, mom, out
                 out=hs_codes[a][:].bitcast(I32), in_=hs_words[a].rearrange("p r i -> p (r i)").bitcast(I32)
             )
 
-        nc.sync.dma_start(out=pairs[0][:].rearrange("p j w -> p (j w)"), in_=run[:, : 2 * N])
+        nc.sync.dma_start(out=last_raw[:].rearrange("p j w -> p (j w)")[:, :cut], in_=run[:, :cut])
         load_hs(0)
-        nc.sync.dma_start(out=pairs[1][:].rearrange("p j w -> p (j w)")[:, : N + COLS], in_=run[:, 2 * N : 3 * N + COLS])
-        nc.sync.dma_start(out=pairs[1][:, 1, COLS:], in_=run[:, 3 * N + COLS :])
+        nc.sync.dma_start(out=last_raw[:].rearrange("p j w -> p (j w)")[:, cut:], in_=run[:, cut:])
         load_hs(1)
 
         mom_sb = []
@@ -177,22 +176,31 @@ def tile_mix_lorab_ema_kernel(tc, x, dn, hs_words, hs_scales, dy0, dy1, mom, out
                 interleave(nc.vector.tensor_copy, dy_g, dy_raw[g], c * COLS, SCALAR_COLS, COLS)
                 groups.append(dy_g)
             for c in range(N_CHUNKS):
-                close_chunk(g, c, groups[c])
+                if (g, c) == (1, LAST):
+                    held = groups[c]
+                elif g == 2:
+                    dy_q[g, c] = quantize("dy%d%d" % (g, c), groups[c], E5M2)
+                else:
+                    close_chunk(g, c, groups[c])
+        close_chunk(1, LAST, held)
+        for rc in early:
+            out_pass(rc, 2)
 
         groups = [new_stage() for c in range(N_CHUNKS)]
 
         def interleave_pair(copy, u, c, lo, hi):
-            interleave(copy, groups[c][:, :, 2 * u : 2 * u + 2], pairs[u], c * COLS, lo, hi)
+            interleave(copy, groups[c][:, :, 2 * u : 2 * u + 2], last_raw[:, 2 * u : 2 * u + 2, :], c * COLS, lo, hi)
 
-        interleave_pair(nc.vector.tensor_copy, 0, 0, 0, COLS)
+        interleave(nc.scalar.copy, groups[0], last_raw, 0, 0, SCALAR_COLS_LAST[0])
+        interleave(nc.vector.tensor_copy, groups[0], last_raw, 0, SCALAR_COLS_LAST[0], COLS)
         interleave_pair(nc.scalar.copy, 0, 1, 0, COLS)
         interleave_pair(nc.vector.tensor_copy, 0, LAST, 0, COLS)
-        for chunks in ([0], range(1, N_CHUNKS)):
-            for c in chunks:
-                interleave_pair(nc.scalar.copy, 1, c, 0, SCALAR_COLS_LAST[c])
-                interleave_pair(nc.vector.tensor_copy, 1, c, SCALAR_COLS_LAST[c], COLS)
-            for c in chunks:
-                close_chunk(3, c, groups[c])
+        close_chunk(3, 0, groups[0])
+        for c in range(1, N_CHUNKS):
+            interleave_pair(nc.scalar.copy, 1, c, 0, SCALAR_COLS_LAST[c])
+            interleave_pair(nc.vector.tensor_copy, 1, c, SCALAR_COLS_LAST[c], COLS)
+        for c in range(1, N_CHUNKS):
+            close_chunk(3, c, groups[c])
 
         waiting = list(late)
         for r in range(R_TILES):
@@ -200,4 +208,4 @@ def tile_mix_lorab_ema_kernel(tc, x, dn, hs_words, hs_scales, dy0, dy1, mom, out
                 finish((r, c))
                 if waiting:
                     run_late(waiting.pop(0), (r, c))
-            nc.scalar.dma_start(out=out[r * P : (r + 1) * P, :], in_=mom_sb[r][:])
+            nc.sync.dma_start(out=out[r * P : (r + 1) * P, :], in_=mom_sb[r][:])

@@ -22,6 +22,7 @@ R_TILES = R // P
 N_CHUNKS = N // COLS
 LAST = N_CHUNKS - 1
 BANKS = 8
+ASIDE_COLS = 256
 MX_ALIGN = 64
 DMA_ALIGN = 256
 SCALAR_COLS = 256
@@ -81,11 +82,14 @@ def tile_mix_lorab_ema_kernel(tc, x, dn, hs_words, hs_scales, dy0, dy1, mom, out
 
         hs_scale_sb = keep.tile([P, 2, R], U8, name="hs_plane", align_bytes=DMA_ALIGN)
         nc.vector.memset(hs_scale_sb[:].bitcast(I32), 0)
-        for i in range(4):
+
+        def load_scale_rows(i):
             nc.sync.dma_start(
                 out=hs_scale_sb[i:P:32, :, :].bitcast(I32),
                 in_=hs_scales.rearrange("a (q i) n -> i q a n", i=4)[i].bitcast(I32),
             )
+
+        load_scale_rows(0)
         dy_raw = [load_passes("dy1_raw%d" % a, dy1[a * ROWS :, :], 1, "dy1_raw%d" % a)[:, 0] for a in range(2)]
 
         dn_q = []
@@ -114,6 +118,8 @@ def tile_mix_lorab_ema_kernel(tc, x, dn, hs_words, hs_scales, dy0, dy1, mom, out
 
         nc.sync.dma_start(out=last_raw[:].rearrange("p j w -> p (j w)")[:, :cut], in_=run[:, :cut])
         load_hs(0)
+        for i in range(1, 4):
+            load_scale_rows(i)
         nc.sync.dma_start(out=last_raw[:].rearrange("p j w -> p (j w)")[:, cut:], in_=run[:, cut:])
         load_hs(1)
 
@@ -150,10 +156,10 @@ def tile_mix_lorab_ema_kernel(tc, x, dn, hs_words, hs_scales, dy0, dy1, mom, out
             r, c = rc
             mx_pass(acc[rc][:], lhs[g], r * P, dy_q[g, c], 0, COLS, E5M2, g == 0, g == 3)
 
-        def finish(rc):
+        def finish(rc, lo):
             r, c = rc
-            part = mom_sb[r][:, c * COLS : (c + 1) * COLS]
-            nc.vector.scalar_tensor_tensor(out=part, in0=part, scalar=0.9, in1=acc[rc][:], op0=ALU.mult, op1=ALU.add)
+            part = mom_sb[r][:, c * COLS + lo : (c + 1) * COLS]
+            nc.vector.scalar_tensor_tensor(out=part, in0=part, scalar=0.9, in1=acc[rc][:, lo:], op0=ALU.mult, op1=ALU.add)
 
         def run_late(rc, freed):
             open_tile(rc, early.index(freed))
@@ -175,14 +181,18 @@ def tile_mix_lorab_ema_kernel(tc, x, dn, hs_words, hs_scales, dy0, dy1, mom, out
                 interleave(nc.scalar.copy, dy_g, dy_raw[g], c * COLS, 0, SCALAR_COLS)
                 interleave(nc.vector.tensor_copy, dy_g, dy_raw[g], c * COLS, SCALAR_COLS, COLS)
                 groups.append(dy_g)
+            if g == 2:
+                close_chunk(1, LAST, held)
+                for rc in early:
+                    if rc[1] == 1:
+                        out_pass(rc, 1)
             for c in range(N_CHUNKS):
                 if (g, c) == (1, LAST):
                     held = groups[c]
-                elif g == 2:
+                elif g == 2 or (g, c) == (1, 1):
                     dy_q[g, c] = quantize("dy%d%d" % (g, c), groups[c], E5M2)
                 else:
                     close_chunk(g, c, groups[c])
-        close_chunk(1, LAST, held)
         for rc in early:
             out_pass(rc, 2)
 
@@ -202,10 +212,20 @@ def tile_mix_lorab_ema_kernel(tc, x, dn, hs_words, hs_scales, dy0, dy1, mom, out
         for c in range(1, N_CHUNKS):
             close_chunk(3, c, groups[c])
 
+        def finish_aside(r):
+            part = mom_sb[r][:, :ASIDE_COLS]
+            emptied = stage.tile([P, ASIDE_COLS], F32, name="emptied", tag="grouped", align_bytes=MX_ALIGN)
+            nc.scalar.copy(out=emptied[:], in_=acc[r, 0][:, :ASIDE_COLS])
+            nc.scalar.mul(out=part, in_=part, mul=0.9)
+            nc.gpsimd.tensor_tensor(out=part, in0=part, in1=emptied[:], op=ALU.add)
+
         waiting = list(late)
         for r in range(R_TILES):
+            helped = (r, 0) in early
+            if helped:
+                finish_aside(r)
             for c in range(N_CHUNKS):
-                finish((r, c))
+                finish((r, c), ASIDE_COLS if helped and c == 0 else 0)
                 if waiting:
                     run_late(waiting.pop(0), (r, c))
             nc.sync.dma_start(out=out[r * P : (r + 1) * P, :], in_=mom_sb[r][:])

@@ -22,11 +22,11 @@ R_TILES = R // P
 N_CHUNKS = N // COLS
 LAST = N_CHUNKS - 1
 BANKS = 8
-ASIDE_COLS = 256
+ASIDE_COLS = 320
 MX_ALIGN = 64
 DMA_ALIGN = 256
 SCALAR_COLS = 256
-SCALAR_COLS_LAST = (192, 128, 384)
+SMALL_SHARE = 128
 STAGE_BUFS = 7
 
 
@@ -198,17 +198,17 @@ def tile_mix_lorab_ema_kernel(tc, x, dn, hs_words, hs_scales, dy0, dy1, mom, out
 
         groups = [new_stage() for c in range(N_CHUNKS)]
 
-        def interleave_pair(copy, u, c, lo, hi):
-            interleave(copy, groups[c][:, :, 2 * u : 2 * u + 2], last_raw[:, 2 * u : 2 * u + 2, :], c * COLS, lo, hi)
+        def interleave_pair(copy, u, lo, hi):
+            interleave(copy, groups[1][:, :, 2 * u : 2 * u + 2], last_raw[:, 2 * u : 2 * u + 2, :], COLS, lo, hi)
 
-        interleave(nc.scalar.copy, groups[0], last_raw, 0, 0, SCALAR_COLS_LAST[0])
-        interleave(nc.vector.tensor_copy, groups[0], last_raw, 0, SCALAR_COLS_LAST[0], COLS)
-        interleave_pair(nc.scalar.copy, 0, 1, 0, COLS)
-        interleave_pair(nc.vector.tensor_copy, 0, LAST, 0, COLS)
+        interleave(nc.scalar.copy, groups[0], last_raw, 0, 0, SMALL_SHARE)
+        interleave(nc.vector.tensor_copy, groups[0], last_raw, 0, SMALL_SHARE, COLS)
+        interleave_pair(nc.scalar.copy, 0, SMALL_SHARE, COLS)
+        interleave_pair(nc.vector.tensor_copy, 0, 0, SMALL_SHARE)
         close_chunk(3, 0, groups[0])
-        for c in range(1, N_CHUNKS):
-            interleave_pair(nc.scalar.copy, 1, c, 0, SCALAR_COLS_LAST[c])
-            interleave_pair(nc.vector.tensor_copy, 1, c, SCALAR_COLS_LAST[c], COLS)
+        interleave_pair(nc.vector.tensor_copy, 1, 0, COLS)
+        interleave(nc.scalar.copy, groups[LAST], last_raw, LAST * COLS, SMALL_SHARE, COLS)
+        interleave(nc.vector.tensor_copy, groups[LAST], last_raw, LAST * COLS, 0, SMALL_SHARE)
         for c in range(1, N_CHUNKS):
             close_chunk(3, c, groups[c])
 

@@ -19,15 +19,12 @@ PACK = 4
 ROWS = P * PACK
 COLS = 512
 R_TILES = R // P
-N_CHUNKS = N // COLS
-LAST = N_CHUNKS - 1
-BANKS = 8
-ASIDE_COLS = 320
 MX_ALIGN = 64
 DMA_ALIGN = 256
-SCALAR_COLS = 256
+SCALAR_COLS = N // 2
 SMALL_SHARE = 128
-STAGE_BUFS = 7
+FIRST_ASIDE = 384
+STAGE_BUFS = 3
 
 
 def tile_mix_lorab_ema_kernel(tc, x, dn, hs_words, hs_scales, dy0, dy1, mom, out):
@@ -39,32 +36,30 @@ def tile_mix_lorab_ema_kernel(tc, x, dn, hs_words, hs_scales, dy0, dy1, mom, out
         psum = ctx.enter_context(tc.psum_pool(name="psum", bufs=1))
         ctx.enter_context(tc.manual_schedule())
 
-        def load_passes(name, src, passes, tag):
-            raw = keep.tile([P, passes, PACK, src.shape[1]], F32, name=name, tag=tag, align_bytes=DMA_ALIGN)
-            nc.sync.dma_start(out=raw[:], in_=src[: passes * ROWS, :].rearrange("(a p j) w -> p a j w", a=passes, j=PACK))
+        def load_pass(name, src, a, tag):
+            raw = keep.tile([P, PACK, src.shape[1]], F32, name=name, tag=tag, align_bytes=DMA_ALIGN)
+            nc.sync.dma_start(out=raw[:], in_=src[a * ROWS : (a + 1) * ROWS, :].rearrange("(p j) w -> p j w", j=PACK))
             return raw
 
-        def new_stage():
-            grouped = stage.tile([P, COLS, PACK], BF16, name="grouped", tag="grouped", align_bytes=MX_ALIGN)
+        def new_stage(width):
+            grouped = stage.tile([P, width, PACK], BF16, name="grouped", tag="grouped", align_bytes=MX_ALIGN)
             return grouped
 
-        def interleave(copy, grouped, raw, first, lo, hi):
-            copy(
-                out=grouped[:, lo:hi, :].rearrange("p (c i) j -> p c j i", i=4),
-                in_=raw[:, :, first + lo : first + hi].rearrange("p j (c i) -> p c j i", i=4),
-            )
+        def interleave(copy, grouped, raw):
+            copy(out=grouped.rearrange("p (c i) j -> p c j i", i=4), in_=raw.rearrange("p j (c i) -> p c j i", i=4))
 
-        def interleave_permuted(copy, grouped, raw, first):
+        def interleave_permuted(copy, grouped, raw):
             copy(
-                out=grouped[:].rearrange("p (s m) j -> p m j s", s=PACK),
-                in_=raw[:, :, first : first + COLS].rearrange("p j (m s) -> p m j s", s=PACK),
+                out=grouped.rearrange("p (s m) j -> p m j s", s=PACK),
+                in_=raw.rearrange("p j (m s) -> p m j s", s=PACK),
             )
 
         def quantize(name, grouped, fmt):
-            codes = keep.tile([P, COLS], U32, name=name + "_codes", align_bytes=MX_ALIGN)
-            scales = keep.tile([P, COLS], U8, name=name + "_scales", align_bytes=MX_ALIGN)
-            nc.vector.quantize_mx(out=codes[:].bitcast(fmt), scales=scales[:], in_=grouped[:].rearrange("p c j -> p (c j)"))
-            return codes, scales
+            width = grouped.shape[1]
+            codes = keep.tile([P, width], U32, name=name + "_codes", align_bytes=MX_ALIGN)
+            scales = keep.tile([P, width], U8, name=name + "_scales", align_bytes=MX_ALIGN)
+            nc.vector.quantize_mx(out=codes[:].bitcast(fmt), scales=scales[:], in_=grouped.rearrange("p c j -> p (c j)"))
+            return [(codes[:, lo : lo + COLS], scales[:, lo : lo + COLS]) for lo in range(0, width, COLS)]
 
         def mx_pass(bank, stationary, m0, moving, n0, n, moving_fmt, start, stop):
             nc.tensor.matmul_mx(
@@ -77,51 +72,48 @@ def tile_mix_lorab_ema_kernel(tc, x, dn, hs_words, hs_scales, dy0, dy1, mom, out
                 stop=stop,
             )
 
-        dn_raw = [load_passes("dn_raw%d" % a, dn[a * ROWS :, :], 1, "dn_raw%d" % a)[:, 0] for a in range(2)]
-        x_raw = [load_passes("x_raw%d" % a, x[a * ROWS :, :], 1, "x_raw%d" % a)[:, 0] for a in range(2)]
-
-        hs_scale_sb = keep.tile([P, 2, R], U8, name="hs_plane", align_bytes=DMA_ALIGN)
-        nc.vector.memset(hs_scale_sb[:].bitcast(I32), 0)
+        hs_plane = keep.tile([P, 2, R], U8, name="hs_plane", align_bytes=DMA_ALIGN)
+        nc.vector.memset(hs_plane[:].bitcast(I32), 0)
 
         def load_scale_rows(i):
             nc.sync.dma_start(
-                out=hs_scale_sb[i:P:32, :, :].bitcast(I32),
+                out=hs_plane[i:P:32, :, :].bitcast(I32),
                 in_=hs_scales.rearrange("a (q i) n -> i q a n", i=4)[i].bitcast(I32),
             )
 
-        load_scale_rows(0)
-        dy_raw = [load_passes("dy1_raw%d" % a, dy1[a * ROWS :, :], 1, "dy1_raw%d" % a)[:, 0] for a in range(2)]
-
-        dn_q = []
+        dn_raw = [load_pass("dn_raw%d" % a, dn, a, "dn_raw%d" % a) for a in range(2)]
+        x_raw = []
+        dy_raw = []
         for a in range(2):
-            dn_g = new_stage()
-            interleave(nc.scalar.copy, dn_g, dn_raw[a], 0, 0, SCALAR_COLS)
-            interleave(nc.vector.tensor_copy, dn_g, dn_raw[a], 0, SCALAR_COLS, COLS)
-            dn_q.append(quantize("dn%d" % a, dn_g, E4M3))
+            x_raw.append(load_pass("x_raw%d" % a, x, a, "x_raw%d" % a))
+            load_scale_rows(a)
+        for a in range(2):
+            dy_raw.append(load_pass("dy1_raw%d" % a, dy1, a, "dy1_raw%d" % a))
+            load_scale_rows(2 + a)
+
+        dn_g = new_stage(2 * R)
+        interleave(nc.scalar.copy, dn_g[:, :R, :], dn_raw[0][:])
+        interleave(nc.vector.tensor_copy, dn_g[:, R:, :], dn_raw[1][:])
+        dn_q = quantize("dn", dn_g[:], E4M3)
+
         x_q = []
         for a in range(2):
-            x_g = [new_stage() for b in range(2)]
-            interleave_permuted(nc.vector.tensor_copy, x_g[0], x_raw[a], 0)
-            interleave_permuted(nc.scalar.copy, x_g[1], x_raw[a], COLS)
-            x_q.append([quantize("x%d%d" % (a, b), x_g[b], E4M3) for b in range(2)])
-        dy_raw.append(load_passes("dy0_raw", dy0, 1, "x_raw0")[:, 0])
+            x_g = new_stage(T)
+            interleave_permuted(nc.vector.tensor_copy, x_g[:, :COLS, :], x_raw[a][:, :, :COLS])
+            interleave_permuted(nc.scalar.copy, x_g[:, COLS:, :], x_raw[a][:, :, COLS:])
+            x_q.append(quantize("x%d" % a, x_g[:], E4M3))
 
+        dy_raw.append(load_pass("dy0_raw", dy0, 0, "x_raw0"))
         run = dy0[ROWS:, :].rearrange("(p j) w -> p (j w)", j=PACK)
-        last_raw = keep.tile([P, PACK, N], F32, name="last_raw", align_bytes=DMA_ALIGN)
+        last_raw = keep.tile([P, PACK, N], F32, name="last_raw", tag="x_raw1", align_bytes=DMA_ALIGN)
+        last_run = last_raw[:].rearrange("p j w -> p (j w)")
         cut = 3 * N + COLS
-        hs_codes = [keep.tile([P, R], U32, name="hs_codes%d" % a, align_bytes=DMA_ALIGN) for a in range(2)]
-
-        def load_hs(a):
-            nc.sync.dma_start(
-                out=hs_codes[a][:].bitcast(I32), in_=hs_words[a].rearrange("p r i -> p (r i)").bitcast(I32)
-            )
-
-        nc.sync.dma_start(out=last_raw[:].rearrange("p j w -> p (j w)")[:, :cut], in_=run[:, :cut])
-        load_hs(0)
-        for i in range(1, 4):
-            load_scale_rows(i)
-        nc.sync.dma_start(out=last_raw[:].rearrange("p j w -> p (j w)")[:, cut:], in_=run[:, cut:])
-        load_hs(1)
+        hs_codes = []
+        for a, part in enumerate((slice(0, cut), slice(cut, PACK * N))):
+            nc.sync.dma_start(out=last_run[:, part], in_=run[:, part])
+            words = keep.tile([P, R], U32, name="hs_codes%d" % a, align_bytes=DMA_ALIGN)
+            nc.sync.dma_start(out=words[:].bitcast(I32), in_=hs_words[a].rearrange("p r i -> p (r i)").bitcast(I32))
+            hs_codes.append(words)
 
         mom_sb = []
         for r in range(R_TILES):
@@ -129,22 +121,21 @@ def tile_mix_lorab_ema_kernel(tc, x, dn, hs_words, hs_scales, dy0, dy1, mom, out
             nc.sync.dma_start(out=m_tile[:], in_=mom[r * P : (r + 1) * P, :])
             mom_sb.append(m_tile)
 
-        lhs = []
-        for b in range(2):
-            h_g = new_stage()
+        h_g = new_stage(2 * R)
+        for b, copy in enumerate((nc.scalar.copy, nc.vector.tensor_copy)):
             for r in range(R_TILES):
                 bank = psum.tile([P, COLS], F32, name="h_bank", tag="bank%d" % (R_TILES * b + r))
                 for s in range(PACK):
                     for a in range(2):
                         mx_pass(bank[:, s * P : (s + 1) * P], x_q[a][b], s * P, dn_q[a], r * P, P, E4M3, a == 0, a == 1)
-                copy = nc.scalar.copy if b == 0 else nc.vector.tensor_copy
-                copy(out=h_g[:, r * P : (r + 1) * P, :], in_=bank[:].rearrange("p (s n) -> p n s", s=PACK))
-            lhs.append(quantize("h%d" % b, h_g, E4M3))
+                first = b * R + r * P
+                copy(out=h_g[:, first : first + P, :], in_=bank[:].rearrange("p (s n) -> p n s", s=PACK))
 
-        lhs.extend((hs_codes[a], hs_scale_sb[:, a, :]) for a in range(2))
+        lhs = quantize("h", h_g[:], E4M3)
+        lhs.extend((hs_codes[a], hs_plane[:, a, :]) for a in range(2))
 
-        tiles = [(r, c) for r in range(R_TILES) for c in range(N_CHUNKS)]
-        early, late = tiles[:BANKS], tiles[BANKS:]
+        early = [(r, 0) for r in range(R_TILES)] + [(r, c) for c in (1, 2) for r in (0, 1)]
+        late = [(r, c) for r in (2, 3) for c in (1, 2)]
         acc = {}
         dy_q = {}
 
@@ -156,76 +147,90 @@ def tile_mix_lorab_ema_kernel(tc, x, dn, hs_words, hs_scales, dy0, dy1, mom, out
             r, c = rc
             mx_pass(acc[rc][:], lhs[g], r * P, dy_q[g, c], 0, COLS, E5M2, g == 0, g == 3)
 
-        def finish(rc, lo):
-            r, c = rc
-            part = mom_sb[r][:, c * COLS + lo : (c + 1) * COLS]
-            nc.vector.scalar_tensor_tensor(out=part, in0=part, scalar=0.9, in1=acc[rc][:, lo:], op0=ALU.mult, op1=ALU.add)
+        def quantize_dy(g, grouped, first, last):
+            done = quantize("dy%d%d" % (g, first), grouped[:, first * COLS : last * COLS, :], E5M2)
+            for c in range(first, last):
+                dy_q[g, c] = done[c - first]
 
-        def run_late(rc, freed):
-            open_tile(rc, early.index(freed))
-            for g in range(4):
-                out_pass(rc, g)
-
-        def close_chunk(g, c, grouped):
-            dy_q[g, c] = quantize("dy%d%d" % (g, c), grouped, E5M2)
-            for rc in early:
-                if rc[1] == c:
-                    out_pass(rc, g)
+        def copy_pass(g):
+            grouped = new_stage(N)
+            interleave(nc.scalar.copy, grouped[:, :SCALAR_COLS, :], dy_raw[g][:, :, :SCALAR_COLS])
+            interleave(nc.vector.tensor_copy, grouped[:, SCALAR_COLS:, :], dy_raw[g][:, :, SCALAR_COLS:])
+            return grouped
 
         for i, rc in enumerate(early):
             open_tile(rc, i)
-        for g in range(3):
-            groups = []
-            for c in range(N_CHUNKS):
-                dy_g = new_stage()
-                interleave(nc.scalar.copy, dy_g, dy_raw[g], c * COLS, 0, SCALAR_COLS)
-                interleave(nc.vector.tensor_copy, dy_g, dy_raw[g], c * COLS, SCALAR_COLS, COLS)
-                groups.append(dy_g)
-            if g == 2:
-                close_chunk(1, LAST, held)
-                for rc in early:
-                    if rc[1] == 1:
-                        out_pass(rc, 1)
-            for c in range(N_CHUNKS):
-                if (g, c) == (1, LAST):
-                    held = groups[c]
-                elif g == 2 or (g, c) == (1, 1):
-                    dy_q[g, c] = quantize("dy%d%d" % (g, c), groups[c], E5M2)
-                else:
-                    close_chunk(g, c, groups[c])
+        grouped = copy_pass(0)
+        quantize_dy(0, grouped, 2, 3)
+        quantize_dy(0, grouped, 0, 2)
+        for rc in early:
+            out_pass(rc, 0)
+        held = copy_pass(1)
+        quantize_dy(1, held, 0, 2)
+        grouped = copy_pass(2)
+        quantize_dy(1, held, 2, 3)
+        for rc in reversed(early):
+            out_pass(rc, 1)
+        quantize_dy(2, grouped, 2, 3)
+        quantize_dy(2, grouped, 0, 2)
         for rc in early:
             out_pass(rc, 2)
 
-        groups = [new_stage() for c in range(N_CHUNKS)]
+        grouped = new_stage(N)
 
-        def interleave_pair(copy, u, lo, hi):
-            interleave(copy, groups[1][:, :, 2 * u : 2 * u + 2], last_raw[:, 2 * u : 2 * u + 2, :], COLS, lo, hi)
+        def copy_last(copy, lo, hi, rows):
+            interleave(copy, grouped[:, lo:hi, rows], last_raw[:, rows, lo:hi])
 
-        interleave(nc.scalar.copy, groups[0], last_raw, 0, 0, SMALL_SHARE)
-        interleave(nc.vector.tensor_copy, groups[0], last_raw, 0, SMALL_SHARE, COLS)
-        interleave_pair(nc.scalar.copy, 0, SMALL_SHARE, COLS)
-        interleave_pair(nc.vector.tensor_copy, 0, 0, SMALL_SHARE)
-        close_chunk(3, 0, groups[0])
-        interleave_pair(nc.vector.tensor_copy, 1, 0, COLS)
-        interleave(nc.scalar.copy, groups[LAST], last_raw, LAST * COLS, SMALL_SHARE, COLS)
-        interleave(nc.vector.tensor_copy, groups[LAST], last_raw, LAST * COLS, 0, SMALL_SHARE)
-        for c in range(1, N_CHUNKS):
-            close_chunk(3, c, groups[c])
+        def close_chunk(c):
+            quantize_dy(3, grouped, c, c + 1)
+            for rc in early:
+                if rc[1] == c:
+                    out_pass(rc, 3)
 
-        def finish_aside(r):
-            part = mom_sb[r][:, :ASIDE_COLS]
-            emptied = stage.tile([P, ASIDE_COLS], F32, name="emptied", tag="grouped", align_bytes=MX_ALIGN)
-            nc.scalar.copy(out=emptied[:], in_=acc[r, 0][:, :ASIDE_COLS])
-            nc.scalar.mul(out=part, in_=part, mul=0.9)
-            nc.gpsimd.tensor_tensor(out=part, in0=part, in1=emptied[:], op=ALU.add)
+        copy_last(nc.scalar.copy, 0, SMALL_SHARE, slice(0, 4))
+        copy_last(nc.vector.tensor_copy, SMALL_SHARE, COLS, slice(0, 4))
+        copy_last(nc.scalar.copy, COLS + SMALL_SHARE, 2 * COLS, slice(0, 2))
+        copy_last(nc.vector.tensor_copy, COLS, COLS + SMALL_SHARE, slice(0, 2))
+        close_chunk(0)
+        copy_last(nc.vector.tensor_copy, COLS, 2 * COLS, slice(2, 4))
+        copy_last(nc.scalar.copy, 2 * COLS + SMALL_SHARE, N, slice(0, 4))
+        copy_last(nc.vector.tensor_copy, 2 * COLS, 2 * COLS + SMALL_SHARE, slice(0, 4))
+        close_chunk(1)
+        close_chunk(2)
 
+        emptied = keep.tile([P, R_TILES, COLS], F32, name="emptied", tag="dn_raw1", align_bytes=DMA_ALIGN)
         waiting = list(late)
-        for r in range(R_TILES):
-            helped = (r, 0) in early
-            if helped:
-                finish_aside(r)
-            for c in range(N_CHUNKS):
-                finish((r, c), ASIDE_COLS if helped and c == 0 else 0)
-                if waiting:
-                    run_late(waiting.pop(0), (r, c))
+
+        def run_late(r):
+            rc = waiting.pop(0)
+            open_tile(rc, r)
+            for g in range(4):
+                out_pass(rc, g)
+
+        def finish(r, c, lo):
+            part = mom_sb[r][:, c * COLS + lo : (c + 1) * COLS]
+            nc.vector.scalar_tensor_tensor(out=part, in0=part, scalar=0.9, in1=acc[r, c][:, lo:], op0=ALU.mult, op1=ALU.add)
+
+        def finish_aside(r, width):
+            part = mom_sb[r][:, :width]
+            nc.scalar.mul(out=part, in_=part, mul=0.9)
+            nc.gpsimd.tensor_tensor(out=part, in0=part, in1=emptied[:, r, :width], op=ALU.add)
+
+        def store(r):
             nc.sync.dma_start(out=out[r * P : (r + 1) * P, :], in_=mom_sb[r][:])
+
+        nc.scalar.copy(out=emptied[:, 0, :FIRST_ASIDE], in_=acc[0, 0][:, :FIRST_ASIDE])
+        finish_aside(0, FIRST_ASIDE)
+        finish(0, 0, FIRST_ASIDE)
+        finish(0, 1, 0)
+        finish(0, 2, 0)
+        store(0)
+        run_late(0)
+        for r in range(1, R_TILES):
+            nc.scalar.copy(out=emptied[:, r, :], in_=acc[r, 0][:])
+            run_late(r)
+        for r in range(1, R_TILES):
+            finish_aside(r, COLS)
+            finish(r, 1, 0)
+            finish(r, 2, 0)
+            store(r)

@@ -23,7 +23,6 @@ MX_ALIGN = 64
 DMA_ALIGN = 256
 SCALAR_COLS = N // 2
 SMALL_SHARE = 128
-FIRST_ASIDE = 384
 STAGE_BUFS = 3
 
 
@@ -198,39 +197,26 @@ def tile_mix_lorab_ema_kernel(tc, x, dn, hs_words, hs_scales, dy0, dy1, mom, out
         close_chunk(1)
         close_chunk(2)
 
-        emptied = keep.tile([P, R_TILES, COLS], F32, name="emptied", tag="dn_raw1", align_bytes=DMA_ALIGN)
-        waiting = list(late)
+        emptied = keep.tile([P, R_TILES - 1, COLS], F32, name="emptied", tag="dn_raw1", align_bytes=DMA_ALIGN)
+        sums = {rc: acc[rc][:] for rc in early}
 
-        def run_late(r):
-            rc = waiting.pop(0)
-            open_tile(rc, r)
+        def run_late(rc, bank):
+            open_tile(rc, bank)
             for g in range(4):
                 out_pass(rc, g)
+            sums[rc] = acc[rc][:]
 
-        def finish(r, c, lo):
-            part = mom_sb[r][:, c * COLS + lo : (c + 1) * COLS]
-            nc.vector.scalar_tensor_tensor(out=part, in0=part, scalar=0.9, in1=acc[r, c][:, lo:], op0=ALU.mult, op1=ALU.add)
+        def finish(r, c):
+            part = mom_sb[r][:, c * COLS : (c + 1) * COLS]
+            nc.vector.scalar_tensor_tensor(out=part, in0=part, scalar=0.9, in1=sums[r, c], op0=ALU.mult, op1=ALU.add)
 
-        def finish_aside(r, width):
-            part = mom_sb[r][:, :width]
-            nc.scalar.mul(out=part, in_=part, mul=0.9)
-            nc.gpsimd.tensor_tensor(out=part, in0=part, in1=emptied[:, r, :width], op=ALU.add)
-
-        def store(r):
+        for r in range(1, R_TILES):
+            nc.scalar.copy(out=emptied[:, r - 1, :], in_=acc[r, 0][:])
+            sums[r, 0] = emptied[:, r - 1, :]
+            run_late(late[r - 1], r)
+        for r in range(R_TILES):
+            for c in range(N // COLS):
+                finish(r, c)
+            if r == 0:
+                run_late(late[-1], 0)
             nc.sync.dma_start(out=out[r * P : (r + 1) * P, :], in_=mom_sb[r][:])
-
-        nc.scalar.copy(out=emptied[:, 0, :FIRST_ASIDE], in_=acc[0, 0][:, :FIRST_ASIDE])
-        finish_aside(0, FIRST_ASIDE)
-        finish(0, 0, FIRST_ASIDE)
-        finish(0, 1, 0)
-        finish(0, 2, 0)
-        store(0)
-        run_late(0)
-        for r in range(1, R_TILES):
-            nc.scalar.copy(out=emptied[:, r, :], in_=acc[r, 0][:])
-            run_late(r)
-        for r in range(1, R_TILES):
-            finish_aside(r, COLS)
-            finish(r, 1, 0)
-            finish(r, 2, 0)
-            store(r)

@@ -75,23 +75,18 @@ def tile_mix_lorab_ema_kernel(tc, x, dn, hs_words, hs_scales, dy0, dy1, mom, out
         nc.vector.memset(hs_plane[:].bitcast(I32), 0)
 
         def load_scale_rows(i):
-            nc.sync.dma_start(
+            nc.scalar.dma_start(
                 out=hs_plane[i:P:32, :, :].bitcast(I32),
                 in_=hs_scales.rearrange("a (q i) n -> i q a n", i=4)[i].bitcast(I32),
             )
 
         dn_raw = [load_pass("dn_raw%d" % a, dn, a, "dn_raw%d" % a) for a in range(2)]
-        x_raw = []
-        dy_raw = []
-        for a in range(2):
-            x_raw.append(load_pass("x_raw%d" % a, x, a, "x_raw%d" % a))
-            load_scale_rows(a)
-        for a in range(2):
-            dy_raw.append(load_pass("dy1_raw%d" % a, dy1, a, "dy1_raw%d" % a))
-            load_scale_rows(2 + a)
+        x_raw = [load_pass("x_raw%d" % a, x, a, "x_raw%d" % a) for a in range(2)]
+        dy_raw = [load_pass("dy1_raw%d" % a, dy1, a, "dy1_raw%d" % a) for a in range(2)]
 
         dn_g = new_stage(2 * R)
         interleave(nc.scalar.copy, dn_g[:, :R, :], dn_raw[0][:])
+        load_scale_rows(0)
         interleave(nc.vector.tensor_copy, dn_g[:, R:, :], dn_raw[1][:])
         dn_q = quantize("dn", dn_g[:], E4M3)
 
@@ -100,6 +95,7 @@ def tile_mix_lorab_ema_kernel(tc, x, dn, hs_words, hs_scales, dy0, dy1, mom, out
             x_g = new_stage(T)
             interleave_permuted(nc.vector.tensor_copy, x_g[:, :COLS, :], x_raw[a][:, :, :COLS])
             interleave_permuted(nc.scalar.copy, x_g[:, COLS:, :], x_raw[a][:, :, COLS:])
+            load_scale_rows(1 + a)
             x_q.append(quantize("x%d" % a, x_g[:], E4M3))
 
         dy_raw.append(load_pass("dy0_raw", dy0, 0, "x_raw0"))
@@ -160,6 +156,7 @@ def tile_mix_lorab_ema_kernel(tc, x, dn, hs_words, hs_scales, dy0, dy1, mom, out
         for i, rc in enumerate(early):
             open_tile(rc, i)
         grouped = copy_pass(0)
+        load_scale_rows(3)
         quantize_dy(0, grouped, 2, 3)
         quantize_dy(0, grouped, 0, 2)
         for rc in early:

from contextlib import ExitStack

import concourse.mybir as mybir

K, O, T, R, N = 1024, 1024, 1024, 512, 1536
FLOPS = 2 * K * T * R + 2 * (O + T) * R * N

F32 = mybir.dt.float32
BF16 = mybir.dt.bfloat16
U32 = mybir.dt.uint32
I32 = mybir.dt.int32
U8 = mybir.dt.uint8
E4M3 = mybir.dt.float8_e4m3fn_x4
E5M2 = mybir.dt.float8_e5m2_x4
ALU = mybir.AluOpType

P = 128
PACK = 4
ROWS = P * PACK
COLS = 512
R_TILES = R // P
MX_ALIGN = 64
DMA_ALIGN = 256
SCALAR_COLS = N // 2
SMALL_SHARE = 128
STAGE_BUFS = 3


def tile_mix_lorab_ema_kernel(tc, x, dn, hs_words, hs_scales, dy0, dy1, mom, out):
    nc = tc.nc

    with ExitStack() as ctx:
        keep = ctx.enter_context(tc.tile_pool(name="keep", bufs=1))
        stage = ctx.enter_context(tc.tile_pool(name="stage", bufs=STAGE_BUFS))
        psum = ctx.enter_context(tc.psum_pool(name="psum", bufs=1))
        ctx.enter_context(tc.manual_schedule())

        def load_pass(name, src, a, tag):
            raw = keep.tile([P, PACK, src.shape[1]], F32, name=name, tag=tag, align_bytes=DMA_ALIGN)
            nc.sync.dma_start(out=raw[:], in_=src[a * ROWS : (a + 1) * ROWS, :].rearrange("(p j) w -> p j w", j=PACK))
            return raw

        def new_stage(width):
            grouped = stage.tile([P, width, PACK], BF16, name="grouped", tag="grouped", align_bytes=MX_ALIGN)
            return grouped

        def interleave(copy, grouped, raw):
            copy(out=grouped.rearrange("p (c i) j -> p c j i", i=4), in_=raw.rearrange("p j (c i) -> p c j i", i=4))

        def interleave_permuted(copy, grouped, raw):
            copy(
                out=grouped.rearrange("p (s m) j -> p m j s", s=PACK),
                in_=raw.rearrange("p j (m s) -> p m j s", s=PACK),
            )

        def quantize(name, grouped, fmt):
            width = grouped.shape[1]
            codes = keep.tile([P, width], U32, name=name + "_codes", align_bytes=MX_ALIGN)
            scales = keep.tile([P, width], U8, name=name + "_scales", align_bytes=MX_ALIGN)
            nc.vector.quantize_mx(out=codes[:].bitcast(fmt), scales=scales[:], in_=grouped.rearrange("p c j -> p (c j)"))
            return [(codes[:, lo : lo + COLS], scales[:, lo : lo + COLS]) for lo in range(0, width, COLS)]

        def mx_pass(bank, stationary, m0, moving, n0, n, moving_fmt, start, stop):
            nc.tensor.matmul_mx(
                out=bank,
                lhsT=stationary[0][:, m0 : m0 + P].bitcast(E4M3),
                lhsT_scale=stationary[1][:, m0 : m0 + P],
                rhs=moving[0][:, n0 : n0 + n].bitcast(moving_fmt),
                rhs_scale=moving[1][:, n0 : n0 + n],
                start=start,
                stop=stop,
            )

        hs_plane = keep.tile([P, 2, R], U8, name="hs_plane", align_bytes=DMA_ALIGN)
        nc.vector.memset(hs_plane[:].bitcast(I32), 0)

        def load_scale_rows(i):
            nc.scalar.dma_start(
                out=hs_plane[i:P:32, :, :].bitcast(I32),
                in_=hs_scales.rearrange("a (q i) n -> i q a n", i=4)[i].bitcast(I32),
            )

        dn_raw = [load_pass("dn_raw%d" % a, dn, a, "dn_raw%d" % a) for a in range(2)]
        x_raw = [load_pass("x_raw%d" % a, x, a, "x_raw%d" % a) for a in range(2)]
        dy_raw = [load_pass("dy1_raw%d" % a, dy1, a, "dy1_raw%d" % a) for a in range(2)]

        dn_g = new_stage(2 * R)
        interleave(nc.scalar.copy, dn_g[:, :R, :], dn_raw[0][:])
        load_scale_rows(0)
        interleave(nc.vector.tensor_copy, dn_g[:, R:, :], dn_raw[1][:])
        dn_q = quantize("dn", dn_g[:], E4M3)

        x_q = []
        for a in range(2):
            x_g = new_stage(T)
            interleave_permuted(nc.vector.tensor_copy, x_g[:, :COLS, :], x_raw[a][:, :, :COLS])
            interleave_permuted(nc.scalar.copy, x_g[:, COLS:, :], x_raw[a][:, :, COLS:])
            load_scale_rows(1 + a)
            x_q.append(quantize("x%d" % a, x_g[:], E4M3))

        dy_raw.append(load_pass("dy0_raw", dy0, 0, "x_raw0"))
        run = dy0[ROWS:, :].rearrange("(p j) w -> p (j w)", j=PACK)
        last_raw = keep.tile([P, PACK, N], F32, name="last_raw", tag="x_raw1", align_bytes=DMA_ALIGN)
        last_run = last_raw[:].rearrange("p j w -> p (j w)")
        cut = 3 * N + COLS
        hs_codes = []
        for a, part in enumerate((slice(0, cut), slice(cut, PACK * N))):
            nc.sync.dma_start(out=last_run[:, part], in_=run[:, part])
            words = keep.tile([P, R], U32, name="hs_codes%d" % a, align_bytes=DMA_ALIGN)
            nc.sync.dma_start(out=words[:].bitcast(I32), in_=hs_words[a].rearrange("p r i -> p (r i)").bitcast(I32))
            hs_codes.append(words)

        mom_sb = []
        for r in range(R_TILES):
            m_tile = keep.tile([P, N], F32, name="mom%d" % r, align_bytes=DMA_ALIGN)
            nc.sync.dma_start(out=m_tile[:], in_=mom[r * P : (r + 1) * P, :])
            mom_sb.append(m_tile)

        h_g = new_stage(2 * R)
        for b, copy in enumerate((nc.scalar.copy, nc.vector.tensor_copy)):
            for r in range(R_TILES):
                bank = psum.tile([P, COLS], F32, name="h_bank", tag="bank%d" % (R_TILES * b + r))
                for s in range(PACK):
                    for a in range(2):
                        mx_pass(bank[:, s * P : (s + 1) * P], x_q[a][b], s * P, dn_q[a], r * P, P, E4M3, a == 0, a == 1)
                first = b * R + r * P
                copy(out=h_g[:, first : first + P, :], in_=bank[:].rearrange("p (s n) -> p n s", s=PACK))

        lhs = quantize("h", h_g[:], E4M3)
        lhs.extend((hs_codes[a], hs_plane[:, a, :]) for a in range(2))

        early = [(r, 0) for r in range(R_TILES)] + [(r, c) for c in (1, 2) for r in (0, 1)]
        late = [(r, c) for r in (2, 3) for c in (1, 2)]
        acc = {}
        dy_q = {}

        def open_tile(rc, i):
            bank = psum.tile([P, COLS], F32, name="acc", tag="bank%d" % i)
            acc[rc] = bank

        def out_pass(rc, g):
            r, c = rc
            mx_pass(acc[rc][:], lhs[g], r * P, dy_q[g, c], 0, COLS, E5M2, g == 0, g == 3)

        def quantize_dy(g, grouped, first, last):
            done = quantize("dy%d%d" % (g, first), grouped[:, first * COLS : last * COLS, :], E5M2)
            for c in range(first, last):
                dy_q[g, c] = done[c - first]

        def copy_pass(g):
            grouped = new_stage(N)
            interleave(nc.scalar.copy, grouped[:, :SCALAR_COLS, :], dy_raw[g][:, :, :SCALAR_COLS])
            interleave(nc.vector.tensor_copy, grouped[:, SCALAR_COLS:, :], dy_raw[g][:, :, SCALAR_COLS:])
            return grouped

        for i, rc in enumerate(early):
            open_tile(rc, i)
        grouped = copy_pass(0)
        load_scale_rows(3)
        quantize_dy(0, grouped, 2, 3)
        quantize_dy(0, grouped, 0, 2)
        for rc in early:
            out_pass(rc, 0)
        held = copy_pass(1)
        quantize_dy(1, held, 0, 2)
        grouped = copy_pass(2)
        quantize_dy(1, held, 2, 3)
        for rc in reversed(early):
            out_pass(rc, 1)
        quantize_dy(2, grouped, 2, 3)
        quantize_dy(2, grouped, 0, 2)
        for rc in early:
            out_pass(rc, 2)

        grouped = new_stage(N)

        def copy_last(copy, lo, hi, rows):
            interleave(copy, grouped[:, lo:hi, rows], last_raw[:, rows, lo:hi])

        def close_chunk(c):
            quantize_dy(3, grouped, c, c + 1)
            for rc in early:
                if rc[1] == c:
                    out_pass(rc, 3)

        copy_last(nc.scalar.copy, 0, SMALL_SHARE, slice(0, 4))
        copy_last(nc.vector.tensor_copy, SMALL_SHARE, COLS, slice(0, 4))
        copy_last(nc.scalar.copy, COLS + SMALL_SHARE, 2 * COLS, slice(0, 2))
        copy_last(nc.vector.tensor_copy, COLS, COLS + SMALL_SHARE, slice(0, 2))
        close_chunk(0)
        copy_last(nc.vector.tensor_copy, COLS, 2 * COLS, slice(2, 4))
        copy_last(nc.scalar.copy, 2 * COLS + SMALL_SHARE, N, slice(0, 4))
        copy_last(nc.vector.tensor_copy, 2 * COLS, 2 * COLS + SMALL_SHARE, slice(0, 4))
        close_chunk(1)
        close_chunk(2)

        emptied = keep.tile([P, R_TILES - 1, COLS], F32, name="emptied", tag="dn_raw1", align_bytes=DMA_ALIGN)
        sums = {rc: acc[rc][:] for rc in early}

        def run_late(rc, bank):
            open_tile(rc, bank)
            for g in range(4):
                out_pass(rc, g)
            sums[rc] = acc[rc][:]

        def finish(r, c):
            part = mom_sb[r][:, c * COLS : (c + 1) * COLS]
            nc.vector.scalar_tensor_tensor(out=part, in0=part, scalar=0.9, in1=sums[r, c], op0=ALU.mult, op1=ALU.add)

        for r in range(1, R_TILES):
            nc.scalar.copy(out=emptied[:, r - 1, :], in_=acc[r, 0][:])
            sums[r, 0] = emptied[:, r - 1, :]
            run_late(late[r - 1], r)
        for r in range(R_TILES):
            for c in range(N // COLS):
                finish(r, c)
            if r == 0:
                run_late(late[-1], 0)
            nc.sync.dma_start(out=out[r * P : (r + 1) * P, :], in_=mom_sb[r][:])
